import numpy as np, ml_dtypes
CORES = [16,17,18,19,32,33,34,35]
N = 8
import mx_ref
BF = ml_dtypes.bfloat16
def entries(a):
    return np.ascontiguousarray(a.T).reshape(-1)
def table(e):
    return np.ascontiguousarray(np.reshape(e, (-1, 16)).T).astype(np.int32)
def cols(t, e):
    v = np.concatenate([t.reshape(128, -1, 4), np.zeros((128, 1, 4), BF)], axis=1)
    return np.ascontiguousarray(v[:, e]).reshape(128, -1)
def cut(t, i, w=512):
    return t[:, w * i:w * i + w]
def f(rng, *shape):
    return mx_ref.flush((rng.standard_normal(shape, dtype=np.float32) * np.exp2(rng.integers(-2, 3, shape[:-1] + (1,)))).astype(BF))
def wide(rng, *shape, cols=0):
    v = rng.standard_normal(shape, dtype=np.float32) * np.exp2(rng.integers(-12, 13, shape)).astype(np.float32)
    if cols: v *= np.repeat(np.exp2(rng.integers(-cols, cols + 1, shape[:-2] + (1, shape[-1] // 4))) * (rng.random(shape[:-2] + (1, shape[-1] // 4)) > 0.0625), 4, axis=-1).astype(np.float32)
    return mx_ref.flush(v.astype(BF))
T, V, M, CAPP, R, O = 512, 192, 288, 32, 3, 2
START = np.repeat(np.arange(N), V)
def loose(rng, at, to, who, but=-1):
    to = to.copy(); n = np.zeros((N, N), int); np.add.at(n, (at, to), 1)
    for i in rng.permutation(who):
        q = rng.integers(0, N)
        if q != but and n[:, q].sum() < M and (q == at[i] or n[at[i], q] < CAPP): n[at[i], to[i]] -= 1; n[at[i], q] += 1; to[i] = q
    return to
def turn(rng, at):
    to = at.copy(); far = 1 + rng.permutation(N - 1)
    for s in range(N):
        k = rng.permutation(np.flatnonzero(at == s))
        for i in range(min(N - 1, len(k) // CAPP)): to[k[CAPP * i:CAPP * i + CAPP]] = (s + far[i]) % N
    return to
def collect(rng, at, e):
    to = at.copy(); k = rng.permutation(np.flatnonzero(at == e))[M - (N - 1) * CAPP:]
    to[k] = (e + 1 + np.arange(len(k)) % (N - 1)) % N
    for s in range(N):
        if s != e: to[rng.permutation(np.flatnonzero(at == s))[:CAPP]] = e
    return to
def spill(rng, at, to, who, ranks):
    to = to.copy(); n = np.zeros((N, N), int); others = np.setdiff1d(np.arange(N * V), who); np.add.at(n, (at[others], to[others]), 1)
    for i in rng.permutation(who):
        q = ranks[np.argmin(np.where(n[at[i], ranks] < CAPP, n[:, ranks].sum(axis=0), N * V))]
        n[at[i], q] += 1; to[i] = q
    return to
def lists(rng, a, share=0.25):
    nx = rng.integers(0, N * T, (N, 2 * T)); free = [list(rng.permutation(2 * T)) for r in range(N)]
    way = np.zeros((R - 1, N * V), int)
    for k in range(R - 2, -1, -1):
        goal = a[k + 1] if k == R - 2 else a[k + 1] * T + way[k + 1] // 2
        known = {}
        for i in rng.permutation(N * V):
            s = int(a[k][i]); L = known.setdefault((s, int(goal[i])), [])
            if not L or rng.random() >= share:
                L.append(free[s].pop()); way[k, i] = L[-1]
            else: way[k, i] = L[rng.integers(0, len(L))]
        if k < R - 2: nx[a[k], way[k]] = goal
    nx[a[R - 2], way[R - 2]] = a[R - 1] * T + rng.integers(0, T, N * V)
    st = (way[0] // 2).reshape(N, V); bt = sum((way[k] % 2) << k for k in range(R - 1)).reshape(N, V)
    return {"nx": np.stack([table(e) for e in nx]), "st": np.stack([table(e) for e in st]), "bt": np.stack([table(e) for e in bt])}
def setup_inputs(rng):
    a = [START]
    for k in range(R - 1): a.append(loose(rng, a[k], a[k], np.arange(N * V)))
    return {"x": f(rng, N, 128, 4 * T), "w": f(rng, N, 128, R * O * 512), **lists(rng, a)}
def setup_inputs_through(rng):
    h = rng.integers(1, N); a = [START, START.copy(), (START + h) % N]
    for s in range(N):
        for g, k in enumerate(np.array_split(V * s + rng.permutation(V), -(-V // CAPP))): a[1][k] = (s + g) % N
    return {**setup_inputs(rng), **lists(rng, a)}
def setup_inputs_far(rng):
    a = [START]
    for k in range(R - 1): a.append(turn(rng, a[k]))
    a[R - 1] = loose(rng, a[R - 2], a[R - 1], np.flatnonzero(a[R - 1] == a[R - 2]))
    return {**setup_inputs(rng), **lists(rng, a)}
def setup_inputs_gather(rng):
    p = rng.permutation(N); home, end, bare = p[:3]; a = [START, START.copy()]
    for j, s in enumerate(p[2:]): a[1][rng.permutation(np.flatnonzero(START == s))[:min(CAPP, max(0, M - V - j * CAPP))]] = home
    to = collect(rng, a[1], end)
    to = spill(rng, a[1], to, np.flatnonzero(((a[1] == end) & (to != end)) | (to == bare)), np.append(p[3:], home))
    a.append(loose(rng, a[1], to, np.flatnonzero((to == a[1]) & (a[1] != end)), but=bare))
    return {**setup_inputs(rng), **lists(rng, a, share=0.75)}
def setup_inputs_stay(rng):
    p = rng.integers(0, N); a = [START, collect(rng, START, p)]
    a.append(loose(rng, a[1], a[1], np.flatnonzero(a[1] != p)))
    return {**setup_inputs(rng), **lists(rng, a)}
def setup_inputs_spread(rng):
    d = setup_inputs(rng); d["x"] = wide(rng, N, 128, 4 * T, cols=8); return d
def follow(nx, st, bt):
    n = np.concatenate([entries(t) for t in nx]); bits = np.concatenate([entries(t) for t in bt])
    at = [np.concatenate([entries(st[r]) + r * T for r in range(N)])]
    for k in range(R - 1): at.append(n[2 * at[k] + (bits >> k & 1)])
    return at
def check_inputs(d):
    b = []
    for name, top in (("nx", N * T), ("st", T), ("bt", 2 ** (R - 1))):
        if d[name].min() < 0 or d[name].max() >= top: b.append(name)
    if b: return b
    at = [t // T for t in follow(d["nx"], d["st"], d["bt"])]
    for k in range(R):
        if np.bincount(at[k], minlength=N).max() > M: b.append("walkers on a rank at step " + str(k))
    for k in range(R - 1):
        n = np.zeros((N, N), int); np.add.at(n, (at[k], at[k + 1]), 1); np.fill_diagonal(n, 0)
        if n.max() > CAPP: b.append("walkers from a rank to another from step " + str(k))
    return b
def reference(x, w, nx, st, bt):
    nodes = np.concatenate([x[r] for r in range(N)], axis=1)
    at = follow(nx, st, bt)
    y = np.zeros((N, 128, O * M), np.float32); ids = np.full((N, 2, M), -1, np.float32)
    for e in range(N):
        m = np.flatnonzero(at[R - 1] // T == e)
        ids[e, 0, :len(m)] = m // V; ids[e, 1, :len(m)] = m % V
        for k in range(R):
            c = np.full(M, -1); c[:len(m)] = at[k][m]
            q = mx_ref.quantize(cols(nodes, c))
            for o in range(O): y[e][:, M * o:M * o + M] += mx_ref.matmul(mx_ref.quantize(np.ascontiguousarray(cut(w[e], k * O + o))), q)
    return {"y": y, "id": ids}

@@ -1,0 +1,442 @@
+from concourse.bass import DstId, RemoteDMATransfer
+from concourse.mybir import dt, AluOpType as A, AxisListType, ActivationFunctionType as F
+
+N = 8
+TN, V, M, KEYS = 512, 192, 288, 1536
+CAP = 32
+ARR = (N - 1) * CAP
+CAND = V + ARR
+ALL = CAND + ARR
+SPREAD = 2 * ARR - 16
+YZ = CAND + SPREAD
+X4 = "float8_e4m3fn_x4"
+
+
+def _sb(n, d="float32"):
+    return ("sbuf", [128, n], d)
+
+
+SCRATCH = {
+    "stw": _sb(12, "int32"), "btw": _sb(12, "int32"), "nxrow": _sb(1024, "int32"), "nxl": _sb(1032, "int32"),
+    "xt": _sb(2048, "bfloat16"), "wt": _sb(3072, "bfloat16"),
+    "ip": _sb(1, "int32"), "ioL": _sb(KEYS), "kL": _sb(208), "wab": _sb(40, "int32"), "cw0": _sb(40), "yx": _sb(ARR),
+    "ci": _sb(16, "int32"), "cf": _sb(16), "wac": _sb(40, "uint16"), "cw": _sb(40), "dw": _sb(40),
+    "o1": _sb(64, "int32"), "off1": _sb(12, "uint16"), "b1u": _sb(12, "uint16"), "stu": _sb(12, "uint16"),
+    "n1r": _sb(V), "n1L": _sb(V), "b1L": _sb(V), "kb": _sb(V), "a1": _sb(V), "aL": _sb(208),
+    "ga": _sb(V), "gb": _sb(V), "c1L": _sb(V), "sg0": _sb(CAND), "sg1": _sb(CAND), "sg2": _sb(CAND), "sg3": _sb(CAND),
+    "cnt1": _sb(2), "i2": _sb(2), "nb": _sb(2), "sub0": _sb(208), "ab1": _sb(208), "vv": _sb(2), "kk": _sb(2),
+    "em": _sb(2), "pk": _sb(2), "x1": _sb(64), "x1t": _sb(64), "w1": _sb(16), "w1i": _sb(14, "int32"), "w1k": _sb(14, "int32"),
+    "s1off": _sb(14, "uint16"), "land1": _sb(14),
+    "own": _sb(V), "ownt": _sb(V), "ow": _sb(96, "int32"), "noff": _sb(26, "uint16"), "c1u": _sb(26, "uint16"),
+    "n2L": _sb(CAND), "g2a": _sb(CAND), "g2b": _sb(CAND), "c2L": _sb(CAND), "l1": _sb(128, "int32"),
+    "cnt2": _sb(8), "x2": _sb(64), "x2t": _sb(64), "w2": _sb(16), "o2off": _sb(28, "uint16"),
+    "ku1": _sb(14, "uint16"), "keyL": _sb(ALL), "inf0": _sb(CAND), "infoL": _sb(424),
+    "xx": _sb(24), "wau": _sb(14, "uint16"), "ig": _sb(ARR), "igt": _sb(ARR), "l2s": _sb(14), "land2": _sb(14),
+    "n2g": _sb(CAND), "n2t": _sb(CAND), "n2w": _sb(112, "int32"), "c2u": _sb(26, "uint16"), "fw": _sb(160),
+    "ko": _sb(40), "kou": _sb(40, "uint16"), "pwa": _sb(40, "uint16"), "ones": _sb(CAND), "bm": _sb(KEYS + ALL), "pp": _sb(KEYS + ALL),
+    "l2i": _sb(64, "int32"), "c2ua": _sb(28, "uint16"), "ku2": _sb(14, "uint16"),
+    "pg": _sb(ALL), "pt": _sb(ALL), "plu": _sb(40, "uint16"), "yx2": _sb(ALL), "tk": _sb(ALL), "inv": _sb(M + ALL, "int32"),
+    "ivg": _sb(M), "ivt": _sb(M), "ivi": _sb(36, "int32"), "ylu": _sb(18, "uint16"),
+    "idk": _sb(2 * M, "int32"), "idf": _sb(3 * M),
+    "xq": _sb(TN, X4), "xs": _sb(TN, "uint8"), "wq": _sb(768, X4), "ws": _sb(768, "uint8"),
+    "stq": _sb(V, X4), "sts": _sb(V, "uint8"), "p1q": _sb(ARR, X4), "p1s": _sb(ARR, "uint8"),
+    "cq": _sb(2 * CAND, X4), "cs": _sb(2 * CAND, "uint8"), "n2q": _sb(CAND, X4), "n2s": _sb(CAND, "uint8"),
+    "p2q": _sb(2 * ARR, X4), "p2s": _sb(2 * ARR, "uint8"), "eq": _sb(2 * ARR, X4), "es": _sb(2 * ARR, "uint8"),
+    "fq": _sb(SPREAD, X4), "fs": _sb(SPREAD, "uint8"),
+    "yb0": _sb(YZ + 8), "yb1": _sb(YZ + 8), "yo0": _sb(M), "yo1": _sb(M),
+    "ps": ("psum", [128, 2048], "float32"),
+}
+SEMAPHORES = ["cv", "cs_", "ct", "cg", "dst", "dbt", "dnx", "dx", "dw_", "dc1", "dc2", "dy0", "dy1", "did", "sent",
+              "al1", "aq1", "as1", "al2", "aq2", "as2"]
+
+
+def _split(core, others, topo):
+    own = topo.cores_of(core)
+    far = [c for c in others if c not in own]
+    near = [c for c in others if c in own]
+    out, taken = {}, []
+    for part in (far, near):
+        if not part:
+            continue
+        free = [e for e in topo.engines(core, part[0]) if e not in taken]
+        k = 1
+        while 2 * k * len(part) <= len(free):
+            k *= 2
+        for j, c in enumerate(part):
+            out[c] = free[j * k:(j + 1) * k]
+            taken += out[c]
+    return out
+
+
+def rank_program(g, core, T, topo):
+    r = T.rank_of(core)
+    if r is None:
+        return
+    sem = T.sem
+    queues = {"v": (g.vector, "cv"), "s": (g.scalar, "cs_"), "t": (g.tensor, "ct"), "g": (g, "cg"), "y": (g.sync, None)}
+    total, seen = {}, {q: {} for q in queues}
+    wrote, read = {}, {}
+
+    def await_(q, toks):
+        eng, need = queues[q][0], {}
+        for s, val in toks:
+            val = total[s] if val is None else val
+            need[s] = max(need.get(s, 0), val)
+        for s in need:
+            if seen[q].get(s, 0) < need[s]:
+                eng.wait_ge(sem[s], need[s])
+                seen[q][s] = need[s]
+
+    def deps(q, r_, w_):
+        mine = queues[q][1]
+        toks = []
+        for k in r_:
+            toks += wrote.get(k, [])
+        for k in w_:
+            toks += [t for t in wrote.get(k, []) + read.get(k, []) if t[0] != mine]
+        await_(q, toks)
+
+    def note(tok, r_, w_):
+        for k in r_:
+            read.setdefault(k, []).append(tok)
+        for k in w_:
+            wrote.setdefault(k, []).append(tok)
+
+    def op(q, r_, w_, fn):
+        r_, w_ = r_.split(), w_.split()
+        deps(q, r_, w_)
+        s = queues[q][1]
+        total[s] = total.get(s, 0) + 1
+        fn(queues[q][0]).then_inc(sem[s], 1)
+        note((s, total[s]), r_, w_)
+
+    def dma(q, s, r_, w_, out, in_):
+        r_, w_ = r_.split(), w_.split()
+        deps(q, r_, w_)
+        total[s] = total.get(s, 0) + 16
+        queues[q][0].dma_start(out, in_).then_inc(sem[s], 16)
+        note((s, None), r_, w_)
+
+    def copy(r_, w_, out, in_, q="v"):
+        if q == "s":
+            op("s", r_, w_, lambda e: e.activation(out, in_, F.Copy))
+        else:
+            op(q, r_, w_, lambda e: e.tensor_copy(out, in_))
+
+    def ts(r_, w_, out, in0, s1, o0, s2=None, o1=None):
+        if o1 is None:
+            op("v", r_, w_, lambda e: e.tensor_scalar(out, in0, s1, None, o0))
+        else:
+            op("v", r_, w_, lambda e: e.tensor_scalar(out, in0, s1, s2, o0, o1))
+
+    def tt(r_, w_, out, a, b, o):
+        op("v", r_, w_, lambda e: e.tensor_tensor(out, a, b, o))
+
+    def fill(w_, ap, c):
+        op("v", "", w_, lambda e: e.memset(ap, c))
+
+    def turn(r_, w_, out, in_):
+        op("v", r_, w_, lambda e: e.transpose(out, in_))
+
+    def iota(w_, ap, pat, base, mult):
+        op("g", "", w_, lambda e: e.iota(ap, pat, base, mult, allow_small_or_imprecise_dtypes=True))
+
+    def pick(deps_q, deps_s, w_q, w_s, oq, os_, iq, is_, off, off_key):
+        copy(deps_q + " " + off_key, w_q, oq.bitcast(dt.uint32), iq.bitcast(dt.uint32).indirect(off))
+        copy(deps_s + " " + off_key, w_s, os_, is_.indirect(off), q="s")
+
+    others = [T.cores[(r + 1 + k) % N] for k in range(N - 1)]
+    engines = _split(core, others, topo)
+
+    def arrivals(s):
+        n = 0
+        for c in others:
+            rc = T.rank_of(c)
+            n += len(_split(c, [T.cores[(rc + 1 + k) % N] for k in range(N - 1)], topo)[core])
+        total[s] = n
+        return (s, n)
+
+    def send(r_, s, src, dst):
+        deps("g", r_.split(), [])
+        tr = []
+        for k, c in enumerate(others):
+            rid, pid = topo.addr(c)[:2]
+            m = 0
+            for e in engines[c]:
+                m |= 1 << e
+            tr.append(RemoteDMATransfer(dst_ids=[DstId(rid=rid, pnc=pid)], dma_engine_mask=m, remote_sem=sem[s],
+                                        src=src(k), dst=dst(N - 2 - k)))
+            total["sent"] = total.get("sent", 0) + len(engines[c])
+        g.remote_dma_fused(tr, local_sem=sem.sent)
+
+    fill("nxrow", T.nxrow[:], 0)
+    for k in range(8):
+        dma("s", "dst", "", "stw", T.stw[16 * k:16 * k + 16, :], T.st[:])
+    for k in range(8):
+        dma("y", "dbt", "", "btw", T.btw[16 * k:16 * k + 16, :], T.bt[:])
+    dma("y", "dnx", "", "nxrow", T.nxrow[0:1, :], T.nx[:])
+    dma("y", "dx", "", "xt", T.xt[:], T.x[:])
+
+    iota("ip", T.ip[:], [[0, 1]], 0, 1)
+    iota("kL", T.kL[:], [[16384, 208]], 0, 0)
+    iota("ioL0", T.ioL[:, 0:512], [[1, 512]], 0, 0)
+    iota("wab", T.wab[:], [[32, 20], [0, 2]], 0, 0)
+    iota("cw0", T.cw0[:], [[16, 40]], 0, 0)
+    ci, cf = T.ci, T.cf
+    c = lambda j: ci[:, j:j + 1]
+    f = lambda j: cf[:, j:j + 1]
+    ts("ip", "c0", c(0), T.ip[:], 1, A.arith_shift_right, 7, A.bitwise_and)
+    ts("ip", "c1", c(1), T.ip[:], 4, A.arith_shift_right, 1, A.bitwise_and)
+    ts("ip", "c2", c(2), T.ip[:], 1, A.bitwise_and)
+    ts("ip", "c3", c(3), T.ip[:], 5, A.arith_shift_right)
+    ts("c0", "c4", c(4), c(0), r + 1, A.add)
+    ts("c2", "c5", c(5), c(2), 16, A.mult)
+    ts("c3", "c6", c(6), c(3), 4, A.mult)
+    ts("c4", "c7", c(7), c(4), 7, A.bitwise_and)
+    tt("c5 c1", "c8", c(8), c(5), c(1), A.add)
+    ts("c7", "lo", f(0), c(7), 512, A.mult)
+    ts("c7", "hi", f(1), c(7), 512, A.mult, 512, A.add)
+    tt("c8 c6", "c9", c(9), c(8), c(6), A.add)
+    ts("c9", "sb", f(2), c(9), -1.0, A.mult, -0.5, A.add)
+    ts("c9", "sb", f(3), c(9), -1.0, A.mult, -2.5, A.add)
+
+    o1 = T.o1
+    ts("btw", "b0", o1[:, 0:12], T.btw[:], 1, A.bitwise_and)
+    ts("btw", "b1", o1[:, 12:24], T.btw[:], 1, A.arith_shift_right)
+    ts("stw", "e0", o1[:, 24:36], T.stw[:], 2, A.mult)
+    copy("b1", "b1u", T.b1u[:], o1[:, 12:24])
+    tt("e0 b0", "e1", o1[:, 36:48], o1[:, 24:36], o1[:, 0:12], A.add)
+    copy("stw", "stu", T.stu[:], T.stw[:])
+    ts("e1", "e2", o1[:, 48:60], o1[:, 36:48], 1025, A.mult)
+    ts("e2", "e3", o1[:, 24:36], o1[:, 48:60], 4, A.arith_shift_right, 1023, A.bitwise_and)
+    copy("e3", "off1", T.off1[:], o1[:, 24:36])
+    copy("nxrow off1", "n1r", T.n1r[:], T.nxrow[:].indirect(T.off1[:]))
+    op("g", "n1r", "n1L", lambda e: e.partition_broadcast(T.n1L[:], T.n1r[0:1, :], 128))
+    fill("nxl", T.nxl[:, 1024:1032], N * TN)
+    op("g", "nxrow", "nxl", lambda e: e.partition_broadcast(T.nxl[:, 0:1024], T.nxrow[0:1, :], 128))
+    copy("ioL0 b1u", "b1L", T.b1L[:], T.ioL[:, 0:8].indirect(T.b1u[:]))
+    tt("b1L kL", "kb", T.kb[:], T.b1L[:], T.kL[:, 0:V], A.add)
+    copy("kL", "aL", T.aL[:, V:208], T.kL[:, V:208])
+    fill("x1", T.x1[:], 0.0)
+    fill("x2", T.x2[:], 0.0)
+    ts("n1L lo", "ga", T.ga[:], T.n1L[:], f(0), A.is_ge)
+    ts("n1L hi", "gb", T.gb[:], T.n1L[:], f(1), A.is_ge)
+    op("v", "ga gb", "c1L", lambda e: e.tensor_tensor_scan(T.c1L[:], T.ga[:], T.gb[:], 0.0, A.add, A.subtract))
+    for k in range(2):
+        op("s", "c1L sb", "cnt1 sgx%d" % k, lambda e: e.activation(T["sg%d" % k][:, 0:V], T.c1L[:], F.Sign, bias=f(2 + k),
+                                                                 accum_out=T.cnt1[:, k:k + 1]))
+    ts("n1L", "a1", T.a1[:], T.n1L[:], 2.0, A.mult)
+    tt("a1 kb", "aL", T.aL[:, 0:V], T.a1[:], T.kb[:], A.add)
+    ts("cnt1", "nb", T.nb[:], T.cnt1[:], 8192.0, A.mult, -16384.0 * 96, A.add)
+    ts("cnt1", "i2", T.i2[:], T.cnt1[:], -0.5, A.mult, 96.0, A.add)
+    op("s", "aL nb", "ab1", lambda e: e.activation(T.ab1[:], T.aL[:], F.Abs, bias=T.nb[:, 1:2]))
+    ts("aL nb", "sub0", T.sub0[:], T.aL[:], T.nb[:, 0:1], A.add)
+    ts("i2", "em", T.em[:], T.i2[:], float(V), A.is_ge, 2047.0, A.mult)
+    ts("i2", "kk", T.kk[:], T.i2[:], float(V * r), A.add)
+    op("v", "sub0", "vv", lambda e: e.tensor_reduce(T.vv[:, 0:1], T.sub0[:], AxisListType.X, A.min, apply_absolute_value=True))
+    tt("kk em", "kk2", T.pk[:], T.kk[:], T.em[:], A.max)
+    op("v", "ab1", "vv", lambda e: e.tensor_reduce(T.vv[:, 1:2], T.ab1[:], AxisListType.X, A.min))
+    ts("kk2", "pk", T.kk[:], T.pk[:], 8192.0, A.mult)
+    tt("pk vv", "x1", T.x1[:, 0:64:32], T.kk[:], T.vv[:], A.add)
+    turn("x1", "x1t", T.x1t[:], T.x1[:])
+    for k in range(8):
+        dma("y" if k % 2 else "s", "dc1", "x1t", "w1", T.w1[16 * k:16 * k + 16, :], T.x1t[0:128:32, :])
+    send("w1", "al1", lambda k: T.w1[:, 2 * k:2 * k + 2], lambda j: T.land1[:, 2 * j:2 * j + 2])
+
+    copy("c1", "odd", f(4), c(1))
+    ts("c1", "even", f(5), c(1), -1.0, A.mult, 1.0, A.add)
+    ts("ip", "c10", c(10), T.ip[:], 15, A.bitwise_and)
+    ts("ip", "c11", c(11), T.ip[:], 31, A.bitwise_and)
+    copy("c10", "q15", f(6), c(10))
+    copy("c11", "q31", f(7), c(11))
+    ts("wab q31", "wac", T.wac[:], T.wab[:], f(7), A.add)
+    ts("cw0 q15", "cw", T.cw[:], T.cw0[:], f(6), A.add)
+    ts("cw", "dw", T.dw[:], T.cw[:], float(KEYS), A.add)
+    copy("n1L wac", "own", T.own[:], T.n1L[:].indirect(T.wac[:, 0:12]), q="s")
+    op("v", "xt", "xq xs", lambda e: e.quantize_mx(T.xq[:], T.xs[:], T.xt[:]))
+    pick("xq", "xs", "stq", "sts", T.stq[:], T.sts[:], T.xq[:], T.xs[:], T.stu[:], "stu")
+    turn("own", "ownt", T.ownt[:], T.own[:])
+    copy("w1", "w1i", T.w1i[:], T.w1[:, 0:14])
+    ts("w1i", "w1k", T.w1k[:], T.w1i[:], 13, A.arith_shift_right)
+    ts("w1k", "s1off", T.s1off[:], T.w1k[:], -V * r, A.add, V - 1, A.min)
+    pick("stq", "sts", "p1q", "p1s", T.p1q[:], T.p1s[:], T.stq[:], T.sts[:], T.s1off[:], "s1off")
+    send("p1q", "aq1", lambda k: T.p1q[:, CAP * k:CAP * k + CAP].bitcast(dt.uint8),
+         lambda j: T.cq[:, V + CAP * j:V + CAP * j + CAP].bitcast(dt.uint8))
+    send("p1s", "as1", lambda k: T.p1s[:, CAP * k:CAP * k + CAP], lambda j: T.cs[:, V + CAP * j:V + CAP * j + CAP])
+    iota("bm", T.bm[:, 0:KEYS], [[0, KEYS]], 0, 0)
+    iota("ones", T.ones[:], [[0, CAND]], 1, 0)
+    deps("y", ["w1"], [])
+    dma("y", "dw_", "", "wt", T.wt[:], T.w[:])
+    ow = T.ow
+    copy("ownt", "n1w", ow[:, 0:12], T.ownt[:, 0:V:16])
+    ts("n1w", "oc", ow[:, 12:24], ow[:, 0:12], 511, A.bitwise_and)
+    ts("n1w", "oa", ow[:, 24:36], ow[:, 0:12], 9, A.arith_shift_right)
+    ts("oc", "od", ow[:, 36:48], ow[:, 12:24], 2, A.mult)
+    ts("oa", "of", ow[:, 48:60], ow[:, 24:36], r, A.not_equal, 1024, A.mult)
+    tt("od b1", "oe", ow[:, 60:72], ow[:, 36:48], o1[:, 12:24], A.add)
+    copy("oc", "c1u0", T.c1u[:, 0:12], ow[:, 12:24])
+    ts("oe", "oe2", ow[:, 72:84], ow[:, 60:72], 1025, A.mult)
+    ts("oe2", "oe3", ow[:, 84:96], ow[:, 72:84], 4, A.arith_shift_right, 1023, A.bitwise_and)
+    tt("oe3 of", "oe4", ow[:, 36:48], ow[:, 84:96], ow[:, 48:60], A.max)
+    copy("oe4", "noff0", T.noff[:, 0:12], ow[:, 36:48])
+    copy("nxl noff0", "n2L0", T.n2L[:, 0:V], T.nxl[:].indirect(T.noff[:, 0:12]))
+    ts("n2L0 lo", "g2a0", T.g2a[:, 0:V], T.n2L[:, 0:V], f(0), A.is_ge)
+    ts("n2L0 hi", "g2b0", T.g2b[:, 0:V], T.n2L[:, 0:V], f(1), A.is_ge)
+    op("v", "g2a0 g2b0", "c2L0", lambda e: e.tensor_tensor_scan(T.c2L[:, 0:V], T.g2a[:, 0:V], T.g2b[:, 0:V], 0.0, A.add, A.subtract))
+    for k in range(2):
+        op("s", "c2L0 sb", "cnt2o sgy%d" % k, lambda e: e.activation(T["sg%d" % (2 + k)][:, 0:V], T.c2L[:, 0:V], F.Sign, bias=f(2 + k),
+                                                                   accum_out=T.cnt2[:, k:k + 1]))
+    op("s", "n2L0", "inf00", lambda e: e.activation(T.inf0[:, 0:V], T.n2L[:, 0:V], F.Copy, scale=2048.0))
+    pick("xq", "xs", "cq0", "cs0", T.cq[:, 0:V], T.cs[:, 0:V], T.xq[:], T.xs[:], T.stu[:], "stu")
+    ts("cnt2o", "cnt2h", T.cnt2[:, 2:4], T.cnt2[:, 0:2], -0.5, A.mult, CAND / 2.0, A.add)
+    pick("xq", "xs", "cq1", "cs1", T.cq[:, CAND:CAND + V], T.cs[:, CAND:CAND + V], T.xq[:], T.xs[:], T.c1u[:, 0:12], "c1u0")
+    ts("ioL0", "keyL", T.keyL[:, 0:V], T.ioL[:, 0:V], float(V * r), A.add)
+    ts("cw", "kw", T.fw[:, 0:12], T.cw[:, 0:12], float(V * r), A.add)
+    for k in range(1, 3):
+        ts("ioL0", "ioL", T.ioL[:, 512 * k:512 * k + 512], T.ioL[:, 0:512], 512.0 * k, A.add)
+    tt("inf00 keyL", "infoL", T.infoL[:, 0:V], T.inf0[:, 0:V], T.keyL[:, 0:V], A.add)
+    fill("infoL", T.infoL[:, CAND:424], 2047.0)
+
+    wrote["land1"] = [arrivals("al1")]
+    wrote["cqa"] = [arrivals("aq1")]
+    wrote["csa"] = [arrivals("as1")]
+    l1 = T.l1
+    copy("land1", "l1", l1[:, 0:14], T.land1[:])
+    ts("l1", "la", l1[:, 14:28], l1[:, 0:14], 1023, A.bitwise_and)
+    ts("l1", "lk", l1[:, 28:42], l1[:, 0:14], 13, A.arith_shift_right)
+    ts("la", "lb", l1[:, 42:56], l1[:, 14:28], 1025, A.mult)
+    ts("lk", "li", l1[:, 56:70], l1[:, 28:42], KEYS, A.is_ge, 1024, A.mult)
+    ts("lb", "lc", l1[:, 70:84], l1[:, 42:56], 4, A.arith_shift_right, 1023, A.bitwise_and)
+    tt("lc li", "ld", l1[:, 84:98], l1[:, 70:84], l1[:, 56:70], A.max)
+    copy("ld", "noff1", T.noff[:, 12:26], l1[:, 84:98])
+    copy("nxl noff1", "n2L1", T.n2L[:, V:CAND], T.nxl[:].indirect(T.noff[:, 12:26]))
+    ts("n2L1 lo", "g2a1", T.g2a[:, V:CAND], T.n2L[:, V:CAND], f(0), A.is_ge)
+    ts("n2L1 hi", "g2b1", T.g2b[:, V:CAND], T.n2L[:, V:CAND], f(1), A.is_ge)
+    op("v", "g2a1 g2b1 c2L0", "c2L1", lambda e: e.tensor_tensor_scan(T.c2L[:, V:CAND], T.g2a[:, V:CAND], T.g2b[:, V:CAND],
+                                                                  T.c2L[:, V - 1:V], A.add, A.subtract))
+    for k in range(2):
+        op("s", "c2L1 sb", "cnt2a sgz%d" % k, lambda e: e.activation(T["sg%d" % (2 + k)][:, V:CAND], T.c2L[:, V:CAND], F.Sign, bias=f(2 + k),
+                                                                   accum_out=T.cnt2[:, 4 + k:5 + k]))
+    ts("l1", "le", l1[:, 98:112], l1[:, 0:14], 1, A.arith_shift_right, 511, A.bitwise_and)
+    ts("lk", "ku1", T.ku1[:], l1[:, 28:42], KEYS - 1, A.min)
+    copy("le", "c1u1", T.c1u[:, 12:26], l1[:, 98:112])
+    ts("cnt2a", "cnt2b", T.cnt2[:, 6:8], T.cnt2[:, 4:6], -0.5, A.mult)
+    tt("cnt2b cnt2h", "x2", T.x2[:, 0:64:32], T.cnt2[:, 6:8], T.cnt2[:, 2:4], A.add)
+    turn("x2", "x2t", T.x2t[:], T.x2[:])
+    for k in range(8):
+        dma("y" if k % 2 else "s", "dc2", "x2t", "w2", T.w2[16 * k:16 * k + 16, :], T.x2t[0:128:32, :])
+    pick("xq", "xs", "cq2", "cs2", T.cq[:, CAND + V:2 * CAND], T.cs[:, CAND + V:2 * CAND], T.xq[:], T.xs[:], T.c1u[:, 12:26], "c1u1")
+    copy("ioL0 ioL ku1", "keyL1", T.keyL[:, V:CAND], T.ioL[:].indirect(T.ku1[:]), q="s")
+    op("s", "n2L1", "inf01", lambda e: e.activation(T.inf0[:, V:CAND], T.n2L[:, V:CAND], F.Copy, scale=2048.0))
+    copy("n2L0 n2L1 wac", "n2g", T.n2g[:], T.n2L[:].indirect(T.wac[:, 0:26]), q="s")
+    tt("inf01 keyL1", "infoL", T.infoL[:, V:CAND], T.inf0[:, V:CAND], T.keyL[:, V:CAND], A.add)
+    ts("w2", "o2off", T.o2off[:, 0:28:2], T.w2[:, 0:14], CAND - 1.0, A.min)
+    ts("w2", "o2off", T.o2off[:, 1:28:2], T.w2[:, 0:14], CAND - 1.0, A.min, float(CAND), A.add)
+    pick("cq0 cq1 cq2 cqa", "cs0 cs1 cs2 csa", "p2q", "p2s", T.p2q[:], T.p2s[:], T.cq[:], T.cs[:], T.o2off[:], "o2off")
+    send("p2q", "aq2", lambda k: T.p2q[:, 64 * k:64 * k + 64].bitcast(dt.uint8),
+         lambda j: T.eq[:, 64 * j:64 * j + 64].bitcast(dt.uint8))
+    send("p2s", "as2", lambda k: T.p2s[:, 64 * k:64 * k + 64], lambda j: T.es[:, 64 * j:64 * j + 64])
+    xx = T.xx
+    ts("w2 even", "xa", xx[:, 0:7], T.w2[:, 0:14:2], f(5), A.mult)
+    ts("w2 odd", "xb", xx[:, 8:15], T.w2[:, 1:14:2], f(4), A.mult)
+    tt("xa xb", "xc", xx[:, 16:23], xx[:, 0:7], xx[:, 8:15], A.add)
+    copy("xc", "wau", T.wau[:, 0:14:2], xx[:, 16:23])
+    copy("xc", "wau", T.wau[:, 1:14:2], xx[:, 16:23])
+    copy("infoL wau", "ig", T.ig[:], T.infoL[:].indirect(T.wau[:]))
+    turn("ig", "igt", T.igt[:], T.ig[:])
+    copy("igt", "l2s", T.l2s[:], T.igt[:, 0:ARR:16])
+    send("l2s", "al2", lambda k: T.l2s[:, 2 * k:2 * k + 2], lambda j: T.land2[:, 2 * j:2 * j + 2])
+    iota("yx", T.yx[:], [[32, 14], [1, 16]], CAND, 0)
+    iota("yx2a", T.yx2[:, 0:CAND], [[2048, CAND]], 256, 0)
+    iota("pp", T.pp[:, KEYS:KEYS + ALL], [[1, ALL]], M + 1, 0)
+    iota("inv", T.inv[:, 0:M], [[0, M]], YZ * 2048 + 256 - V - 1, 0)
+
+    turn("n2g", "n2t", T.n2t[:], T.n2g[:])
+    n2w, fw = T.n2w, T.fw
+    copy("n2t", "n2w", n2w[:, 0:26], T.n2t[:, 0:CAND:16])
+    ts("lk", "kw", fw[:, 12:26], l1[:, 28:42], KEYS - 1, A.min)
+    ts("n2w", "n2e", n2w[:, 52:78], n2w[:, 0:26], 9, A.arith_shift_right)
+    ts("n2w", "n2c", n2w[:, 26:52], n2w[:, 0:26], 511, A.bitwise_and)
+    ts("n2e", "bad", fw[:, 40:66], n2w[:, 52:78], r, A.not_equal)
+    copy("n2c", "c2u", T.c2u[:], n2w[:, 26:52])
+    tt("bad dw", "badd", fw[:, 80:106], fw[:, 40:66], T.dw[:, 0:26], A.mult)
+    pick("xq", "xs", "n2q", "n2s", T.n2q[:], T.n2s[:], T.xq[:], T.xs[:], T.c2u[:], "c2u")
+    tt("kw badd", "ko0", T.ko[:, 0:26], fw[:, 0:26], fw[:, 80:106], A.max)
+    op("v", "wt", "wq0 ws0", lambda e: e.quantize_mx(T.wq[:, 0:384], T.ws[:, 0:384], T.wt[:, 0:1536]))
+    copy("ko0", "kou0", T.kou[:, 0:26], T.ko[:, 0:26])
+    op("v", "wt", "wq1 ws1", lambda e: e.quantize_mx(T.wq[:, 384:768], T.ws[:, 384:768], T.wt[:, 1536:3072]))
+    op("v", "kou0 ones", "bm", lambda e: e.tensor_copy(T.bm[:].indirect(T.kou[:, 0:26]), T.ones[:]))
+
+    W = lambda k, o: (T.wq[:, 128 * (2 * k + o):128 * (2 * k + o) + 128], T.ws[:, 128 * (2 * k + o):128 * (2 * k + o) + 128])
+
+    def mm(r_, w_, bank, n, k, o, q, s, a, b):
+        wq, ws = W(k, o)
+        op("t", r_ + " wq0 ws0 wq1 ws1", w_, lambda e: e.matmul_mx(T.ps[:, 512 * bank:512 * bank + n], wq, ws, q, s, a, b))
+
+    for o in range(2):
+        mm("cq0 cqa cs0 csa", "psS%d" % o, o, CAND, 0, o, T.cq[:, 0:CAND], T.cs[:, 0:CAND], True, False)
+        mm("cq1 cq2 cs1 cs2", "psS%d" % o, o, CAND, 1, o, T.cq[:, CAND:2 * CAND], T.cs[:, CAND:2 * CAND], False, False)
+        mm("n2q n2s", "psS%d" % o, o, CAND, 2, o, T.n2q[:], T.n2s[:], False, True)
+    tt("yx2a keyL keyL1", "tk0", T.tk[:, 0:CAND], T.yx2[:, 0:CAND], T.keyL[:, 0:CAND], A.add)
+    ts("yx", "yx2b", T.yx2[:, CAND:ALL], T.yx[:], 2048.0, A.mult, 256.0, A.add)
+    for o in range(2):
+        fill("yb%d" % o, T["yb%d" % o][:, YZ:YZ + 8], 0.0)
+
+    wrote["land2"] = [arrivals("al2")]
+    wrote["eqa"] = [arrivals("aq2")]
+    wrote["esa"] = [arrivals("as2")]
+    l2 = T.l2i
+    copy("land2", "m0", l2[:, 0:14], T.land2[:])
+    ts("m0", "m1", l2[:, 14:28], l2[:, 0:14], 2047, A.bitwise_and)
+    ts("m0", "m2", l2[:, 28:42], l2[:, 0:14], 11, A.arith_shift_right, 511, A.bitwise_and)
+    ts("m1", "m3", fw[:, 106:120], l2[:, 14:28], KEYS, A.is_ge)
+    ts("m1", "m4", fw[:, 120:134], l2[:, 14:28], KEYS - 1, A.min)
+    ts("m1", "ku2", T.ku2[:], l2[:, 14:28], KEYS - 1, A.min)
+    tt("m3 dw", "m5", fw[:, 134:148], fw[:, 106:120], T.dw[:, 26:40], A.mult)
+    copy("m2", "c2ua", T.c2ua[:, 0:28:2], l2[:, 28:42])
+    copy("m2", "c2ua", T.c2ua[:, 1:28:2], l2[:, 28:42])
+    tt("m4 m5", "ko1", T.ko[:, 26:40], fw[:, 120:134], fw[:, 134:148], A.max)
+    copy("ko1", "kou1", T.kou[:, 26:40], T.ko[:, 26:40])
+    op("v", "kou1 ones", "bm", lambda e: e.tensor_copy(T.bm[:].indirect(T.kou[:, 26:40]), T.ones[:, 0:ARR]))
+    copy("ioL0 ioL ku2", "keyL2", T.keyL[:, CAND:ALL], T.ioL[:].indirect(T.ku2[:]), q="s")
+    pick("xq", "xs", "fq", "fs", T.fq[:], T.fs[:], T.xq[:], T.xs[:], T.c2ua[:, 0:27], "c2ua")
+    for o in range(2):
+        copy("psS%d" % o, "yb%d" % o, T["yb%d" % o][:, 0:CAND], T.ps[:, 512 * o:512 * o + CAND], q="s")
+    for o in range(2):
+        mm("fq fs", "psA%d" % o, 2 + o, SPREAD, 2, o, T.fq[:], T.fs[:], True, False)
+    ts("ko0 ko1 even", "q0", fw[:, 0:20], T.ko[:, 0:40:2], f(5), A.mult)
+    ts("ko0 ko1 odd", "q1", fw[:, 20:40], T.ko[:, 1:40:2], f(4), A.mult)
+    op("v", "bm", "pp", lambda e: e.tensor_tensor_scan(T.pp[:, 0:KEYS], T.bm[:, 0:KEYS], T.bm[:, 0:KEYS], 0.0, A.add, A.max))
+    tt("q0 q1", "q2", fw[:, 40:60], fw[:, 0:20], fw[:, 20:40], A.add)
+    copy("q2", "pwa", T.pwa[:, 0:40:2], fw[:, 40:60])
+    copy("q2", "pwa", T.pwa[:, 1:40:2], fw[:, 40:60])
+    copy("pp pwa", "pg", T.pg[:], T.pp[:].indirect(T.pwa[:]))
+    turn("pg", "pt", T.pt[:], T.pg[:])
+    tt("yx2b keyL2", "tk1", T.tk[:, CAND:ALL], T.yx2[:, CAND:ALL], T.keyL[:, CAND:ALL], A.add)
+    ts("pt", "plu", T.plu[:], T.pt[:, 0:ALL:16], -1.0, A.add)
+    op("v", "plu tk0 tk1", "inv", lambda e: e.tensor_copy(T.inv[:].indirect(T.plu[:]), T.tk[:]))
+    copy("inv wac", "ivg", T.ivg[:], T.inv[:, 0:M].indirect(T.wac[:, 0:18]))
+    turn("ivg", "ivt", T.ivt[:], T.ivg[:])
+    copy("ivt", "ivi", T.ivi[:, 0:18], T.ivt[:, 0:M:16])
+    ts("ivi", "ivj", T.ivi[:, 18:36], T.ivi[:, 0:18], 11, A.arith_shift_right)
+    copy("ivj", "ylu", T.ylu[:], T.ivi[:, 18:36])
+    for o in range(2):
+        mm("eqa esa", "psA%d" % o, 2 + o, SPREAD, 0, o, T.eq[:, 0:SPREAD], T.es[:, 0:SPREAD], False, False)
+        mm("eqa esa", "psA%d" % o, 2 + o, SPREAD, 1, o, T.eq[:, 16:16 + SPREAD], T.es[:, 16:16 + SPREAD], False, True)
+    ik, fd = T.idk, T.idf
+    I = lambda j: ik[:, M * j:M * j + M]
+    D = lambda j: fd[:, M * j:M * j + M]
+    ts("inv", "i1", I(0), T.inv[:, 0:M], 2047, A.bitwise_and)
+    ts("i1", "i2x", I(1), I(0), 1.0 / V, A.mult, -255.5 / V - 0.5, A.add)
+    ts("i2x", "d0", D(0), I(1), -1.0, A.max)
+    ts("d0", "d1", D(1), D(0), -float(V), A.mult, -256.0, A.add)
+    tt("d1 i1", "d2", D(2), D(1), I(0), A.add)
+    dma("y", "did", "d0", "id0", T["id"][0:1, :], fd[0:1, 0:M])
+    dma("y", "did", "d2", "id1", T["id"][1:2, :], fd[0:1, 2 * M:3 * M])
+    copy("psA0", "yb0", T.yb0[:, CAND:YZ], T.ps[:, 1024:1024 + SPREAD])
+    copy("psA1", "yb1", T.yb1[:, CAND:YZ], T.ps[:, 1536:1536 + SPREAD], q="s")
+    copy("yb0 ylu", "yo0", T.yo0[:], T.yb0[:].indirect(T.ylu[:]))
+    copy("yb1 ylu", "yo1", T.yo1[:], T.yb1[:].indirect(T.ylu[:]), q="s")
+    dma("y", "dy0", "yo0", "y0", T.y[:, 0:M], T.yo0[:])
+    dma("s", "dy1", "yo1", "y1", T.y[:, M:2 * M], T.yo1[:])
+    await_("g", [(s, None) for s in total])

@@ -6,9 +6,12 @@ TN, V, M, KEYS = 512, 192, 288, 1536
 CAP = 32
 ARR = (N - 1) * CAP
 CAND = V + ARR
+CX = CAND + CAP
 ALL = CAND + ARR
+TAIL = CAND + N * CAP
 SPREAD = 2 * ARR - 16
 YZ = CAND + SPREAD
+KW = 1544
 X4 = "float8_e4m3fn_x4"
 
 
@@ -17,37 +20,36 @@ def _sb(n, d="float32"):
 
 
 SCRATCH = {
-    "stw": _sb(12, "int32"), "btw": _sb(12, "int32"), "nxrow": _sb(1024, "int32"), "nxl": _sb(1032, "int32"),
-    "xt": _sb(2048, "bfloat16"), "wt": _sb(3072, "bfloat16"),
-    "ip": _sb(1, "int32"), "ioL": _sb(KEYS), "kL": _sb(208), "wab": _sb(40, "int32"), "cw0": _sb(40), "yx": _sb(ARR),
-    "ci": _sb(16, "int32"), "cf": _sb(16), "wac": _sb(40, "uint16"), "cw": _sb(40), "dw": _sb(40),
+    "stw": _sb(12, "int32"), "btw": _sb(12, "int32"), "nxrow": _sb(1024, "int32"), "nxw": _sb(64, "int32"), "nxf": _sb(64),
+    "nxt": _sb(64), "nxlin": _sb(1024), "nxl": _sb(1032), "xt": _sb(2048, "bfloat16"), "wt": _sb(3072, "bfloat16"),
+    "ic": _sb(160), "ict": _sb(160), "cf": _sb(16), "ioL": _sb(KW), "kL": _sb(208), "wab": _sb(40, "int32"), "cw0": _sb(40),
+    "wac": _sb(40, "uint16"), "cw": _sb(40), "dw": _sb(40), "yx": _sb(ALL), "sT": _sb(KW), "iT": _sb(KW),
     "o1": _sb(64, "int32"), "off1": _sb(12, "uint16"), "b1u": _sb(12, "uint16"), "stu": _sb(12, "uint16"),
     "n1r": _sb(V), "n1L": _sb(V), "b1L": _sb(V), "kb": _sb(V), "a1": _sb(V), "aL": _sb(208),
-    "ga": _sb(V), "gb": _sb(V), "c1L": _sb(V), "sg0": _sb(CAND), "sg1": _sb(CAND), "sg2": _sb(CAND), "sg3": _sb(CAND),
-    "cnt1": _sb(2), "i2": _sb(2), "nb": _sb(2), "sub0": _sb(208), "ab1": _sb(208), "vv": _sb(2), "kk": _sb(2),
-    "em": _sb(2), "pk": _sb(2), "x1": _sb(64), "x1t": _sb(64), "w1": _sb(16), "w1i": _sb(14, "int32"), "w1k": _sb(14, "int32"),
-    "s1off": _sb(14, "uint16"), "land1": _sb(14),
+    "ga": _sb(V), "gb": _sb(V), "c1L": _sb(V), "sg0": _sb(V), "sg1": _sb(V), "sg2": _sb(CX), "sg3": _sb(CX),
+    "cnt1": _sb(2), "nb": _sb(2), "sub0": _sb(208), "ab1": _sb(208), "vv": _sb(2), "pk": _sb(2),
+    "x1": _sb(64), "x1t": _sb(64), "w1": _sb(16), "w1i": _sb(16, "int32"), "w1k": _sb(16, "int32"),
+    "s1off": _sb(16, "uint16"), "land1": _sb(14),
     "own": _sb(V), "ownt": _sb(V), "ow": _sb(96, "int32"), "noff": _sb(26, "uint16"), "c1u": _sb(26, "uint16"),
-    "n2L": _sb(CAND), "g2a": _sb(CAND), "g2b": _sb(CAND), "c2L": _sb(CAND), "l1": _sb(128, "int32"),
-    "cnt2": _sb(8), "x2": _sb(64), "x2t": _sb(64), "w2": _sb(16), "o2off": _sb(28, "uint16"),
-    "ku1": _sb(14, "uint16"), "keyL": _sb(ALL), "inf0": _sb(CAND), "infoL": _sb(424),
-    "xx": _sb(24), "wau": _sb(14, "uint16"), "ig": _sb(ARR), "igt": _sb(ARR), "l2s": _sb(14), "land2": _sb(14),
-    "n2g": _sb(CAND), "n2t": _sb(CAND), "n2w": _sb(112, "int32"), "c2u": _sb(26, "uint16"), "fw": _sb(160),
-    "ko": _sb(40), "kou": _sb(40, "uint16"), "pwa": _sb(40, "uint16"), "ones": _sb(CAND), "bm": _sb(KEYS + ALL), "pp": _sb(KEYS + ALL),
-    "l2i": _sb(64, "int32"), "c2ua": _sb(28, "uint16"), "ku2": _sb(14, "uint16"),
-    "pg": _sb(ALL), "pt": _sb(ALL), "plu": _sb(40, "uint16"), "yx2": _sb(ALL), "tk": _sb(ALL), "inv": _sb(M + ALL, "int32"),
-    "ivg": _sb(M), "ivt": _sb(M), "ivi": _sb(36, "int32"), "ylu": _sb(18, "uint16"),
-    "idk": _sb(2 * M, "int32"), "idf": _sb(3 * M),
+    "n2L": _sb(CAND), "g2a": _sb(CAND), "g2b": _sb(CAND), "c2L": _sb(CX), "l1": _sb(64, "int32"),
+    "cnt2": _sb(8), "x2": _sb(64), "x2t": _sb(64), "w2": _sb(16), "o2off": _sb(32, "uint16"), "w2u": _sb(16, "uint16"),
+    "ku1": _sb(14, "uint16"), "keyL": _sb(CAND), "inf0": _sb(CAND), "infoL": _sb(CX),
+    "ig": _sb(256), "ig2": _sb(256), "igt": _sb(256), "l2s": _sb(16), "land2": _sb(14),
+    "n2g": _sb(CAND), "n2t": _sb(CAND), "n2w": _sb(80, "int32"), "c2u": _sb(26, "uint16"), "fw": _sb(120), "xx": _sb(60),
+    "ko": _sb(26), "kou": _sb(40, "uint16"), "pwa": _sb(40, "uint16"), "ones": _sb(CAND), "bm": _sb(KEYS + TAIL), "pp": _sb(KEYS + TAIL),
+    "l2i": _sb(64, "int32"), "c2ua": _sb(28, "uint16"), "ku2": _sb(28, "uint16"), "sW": _sb(YZ + 8), "iW": _sb(YZ + 8),
+    "pg": _sb(ALL), "pt": _sb(ALL), "plu": _sb(40, "uint16"), "inv": _sb(M + TAIL),
+    "ivg": _sb(M), "ivt": _sb(M), "ylu": _sb(18, "uint16"), "ids": _sb(M), "idi": _sb(M),
     "xq": _sb(TN, X4), "xs": _sb(TN, "uint8"), "wq": _sb(768, X4), "ws": _sb(768, "uint8"),
-    "stq": _sb(V, X4), "sts": _sb(V, "uint8"), "p1q": _sb(ARR, X4), "p1s": _sb(ARR, "uint8"),
+    "stq": _sb(V, X4), "sts": _sb(V, "uint8"), "p1q": _sb(256, X4), "p1s": _sb(256, "uint8"),
     "cq": _sb(2 * CAND, X4), "cs": _sb(2 * CAND, "uint8"), "n2q": _sb(CAND, X4), "n2s": _sb(CAND, "uint8"),
-    "p2q": _sb(2 * ARR, X4), "p2s": _sb(2 * ARR, "uint8"), "eq": _sb(2 * ARR, X4), "es": _sb(2 * ARR, "uint8"),
+    "p2q": _sb(512, X4), "p2s": _sb(512, "uint8"), "eq": _sb(2 * ARR, X4), "es": _sb(2 * ARR, "uint8"),
     "fq": _sb(SPREAD, X4), "fs": _sb(SPREAD, "uint8"),
     "yb0": _sb(YZ + 8), "yb1": _sb(YZ + 8), "yo0": _sb(M), "yo1": _sb(M),
     "ps": ("psum", [128, 2048], "float32"),
 }
-SEMAPHORES = ["cv", "cs_", "ct", "cg", "dst", "dbt", "dnx", "dx", "dw_", "dc1", "dc2", "dy0", "dy1", "did", "sent",
-              "al1", "aq1", "as1", "al2", "aq2", "as2"]
+SEMAPHORES = ["cv", "cs_", "ct", "cg", "dst", "dbt", "dnx", "dnw", "dnl", "dx", "dw_", "dcq", "dc1", "dc2", "dy0", "dy1", "did",
+              "did2", "sent", "al1", "aq1", "as1", "al2", "aq2", "as2"]
 
 
 def _split(core, others, topo):
@@ -87,13 +89,13 @@ def rank_program(g, core, T, topo):
                 eng.wait_ge(sem[s], need[s])
                 seen[q][s] = need[s]
 
-    def deps(q, r_, w_):
-        mine = queues[q][1]
+    def deps(q, r_, w_, own=None):
+        mine = (queues[q][1], own)
         toks = []
         for k in r_:
             toks += wrote.get(k, [])
         for k in w_:
-            toks += [t for t in wrote.get(k, []) + read.get(k, []) if t[0] != mine]
+            toks += [t for t in wrote.get(k, []) + read.get(k, []) if t[0] not in mine]
         await_(q, toks)
 
     def note(tok, r_, w_):
@@ -112,14 +114,15 @@ def rank_program(g, core, T, topo):
 
     def dma(q, s, r_, w_, out, in_):
         r_, w_ = r_.split(), w_.split()
-        deps(q, r_, w_)
+        deps(q, r_, w_, s)
         total[s] = total.get(s, 0) + 16
         queues[q][0].dma_start(out, in_).then_inc(sem[s], 16)
         note((s, None), r_, w_)
 
-    def copy(r_, w_, out, in_, q="v"):
+    def copy(r_, w_, out, in_, q="v", scale=1.0):
         if q == "s":
-            op("s", r_, w_, lambda e: e.activation(out, in_, F.Copy))
+            op("s", r_, w_, (lambda e: e.activation(out, in_, F.Copy)) if scale == 1.0 else
+               (lambda e: e.activation(out, in_, F.Copy, scale=scale)))
         else:
             op(q, r_, w_, lambda e: e.tensor_copy(out, in_))
 
@@ -138,234 +141,230 @@ def rank_program(g, core, T, topo):
     def turn(r_, w_, out, in_):
         op("v", r_, w_, lambda e: e.transpose(out, in_))
 
-    def iota(w_, ap, pat, base, mult):
+    def iota(w_, ap, pat, base, mult=0):
         op("g", "", w_, lambda e: e.iota(ap, pat, base, mult, allow_small_or_imprecise_dtypes=True))
+
+    def count(r_, w_, out, in_, bias, acc):
+        op("s", r_, w_, lambda e: e.activation(out, in_, F.Sign, bias=bias, accum_out=acc))
+
+    def scan(r_, w_, out, a, b, init, o1):
+        op("v", r_, w_, lambda e: e.tensor_tensor_scan(out, a, b, init, A.add, o1))
 
     def pick(deps_q, deps_s, w_q, w_s, oq, os_, iq, is_, off, off_key):
         copy(deps_q + " " + off_key, w_q, oq.bitcast(dt.uint32), iq.bitcast(dt.uint32).indirect(off))
         copy(deps_s + " " + off_key, w_s, os_, is_.indirect(off), q="s")
 
-    others = [T.cores[(r + 1 + k) % N] for k in range(N - 1)]
+    others = [c for c in T.cores if c != core]
     engines = _split(core, others, topo)
 
     def arrivals(s):
-        n = 0
-        for c in others:
-            rc = T.rank_of(c)
-            n += len(_split(c, [T.cores[(rc + 1 + k) % N] for k in range(N - 1)], topo)[core])
+        n = sum(len(_split(c, [b for b in T.cores if b != c], topo)[core]) for c in others)
         total[s] = n
         return (s, n)
 
     def send(r_, s, src, dst):
         deps("g", r_.split(), [])
         tr = []
-        for k, c in enumerate(others):
+        for c in others:
+            d = T.rank_of(c)
             rid, pid = topo.addr(c)[:2]
             m = 0
             for e in engines[c]:
                 m |= 1 << e
             tr.append(RemoteDMATransfer(dst_ids=[DstId(rid=rid, pnc=pid)], dma_engine_mask=m, remote_sem=sem[s],
-                                        src=src(k), dst=dst(N - 2 - k)))
+                                        src=src(d), dst=dst(r - (r > d))))
             total["sent"] = total.get("sent", 0) + len(engines[c])
         g.remote_dma_fused(tr, local_sem=sem.sent)
 
     fill("nxrow", T.nxrow[:], 0)
     for k in range(8):
         dma("s", "dst", "", "stw", T.stw[16 * k:16 * k + 16, :], T.st[:])
-    for k in range(8):
         dma("y", "dbt", "", "btw", T.btw[16 * k:16 * k + 16, :], T.bt[:])
+    for k in range(2):
+        dma("s", "dnw", "", "nxw", T.nxw[16 * k:16 * k + 16, :], T.nx[:])
     dma("y", "dnx", "", "nxrow", T.nxrow[0:1, :], T.nx[:])
     dma("y", "dx", "", "xt", T.xt[:], T.x[:])
 
-    iota("ip", T.ip[:], [[0, 1]], 0, 1)
-    iota("kL", T.kL[:], [[16384, 208]], 0, 0)
-    iota("ioL0", T.ioL[:, 0:512], [[1, 512]], 0, 0)
-    iota("wab", T.wab[:], [[32, 20], [0, 2]], 0, 0)
-    iota("cw0", T.cw0[:], [[16, 40]], 0, 0)
-    ci, cf = T.ci, T.cf
-    c = lambda j: ci[:, j:j + 1]
+    ic, ict, cf, fw = T.ic, T.ict, T.cf, T.fw
+    iota("ic", ic[:, 0:32], [[0, 2], [512, 8], [0, 2]], 0)
+    iota("ic", ic[:, 32:64], [[8, 2], [0, 8], [128, 2]], 4, 1)
+    iota("ic", ic[:, 64:96], [[1, 2], [0, 16]], 0)
+    iota("ic", ic[:, 96:128], [[0, 2], [1, 16]], 0)
+    iota("ic", ic[:, 128:160], [[1, 32]], 0)
+    iota("kL", T.kL[:], [[16384, 208]], 0)
+    iota("ioL0", T.ioL[:, 0:256], [[1, 256]], 0)
+    iota("wab", T.wab[:], [[32, 20], [0, 2]], 0)
+    iota("cw0", T.cw0[:], [[16, 40]], 0)
+    turn("ic", "ict", ict[:], ic[:])
     f = lambda j: cf[:, j:j + 1]
-    ts("ip", "c0", c(0), T.ip[:], 1, A.arith_shift_right, 7, A.bitwise_and)
-    ts("ip", "c1", c(1), T.ip[:], 4, A.arith_shift_right, 1, A.bitwise_and)
-    ts("ip", "c2", c(2), T.ip[:], 1, A.bitwise_and)
-    ts("ip", "c3", c(3), T.ip[:], 5, A.arith_shift_right)
-    ts("c0", "c4", c(4), c(0), r + 1, A.add)
-    ts("c2", "c5", c(5), c(2), 16, A.mult)
-    ts("c3", "c6", c(6), c(3), 4, A.mult)
-    ts("c4", "c7", c(7), c(4), 7, A.bitwise_and)
-    tt("c5 c1", "c8", c(8), c(5), c(1), A.add)
-    ts("c7", "lo", f(0), c(7), 512, A.mult)
-    ts("c7", "hi", f(1), c(7), 512, A.mult, 512, A.add)
-    tt("c8 c6", "c9", c(9), c(8), c(6), A.add)
-    ts("c9", "sb", f(2), c(9), -1.0, A.mult, -0.5, A.add)
-    ts("c9", "sb", f(3), c(9), -1.0, A.mult, -2.5, A.add)
+    lo, odd, q15, q31 = (ict[:, j:j + 1] for j in (0, 64, 96, 128))
+    ts("ict", "hi", f(1), lo, 512.0, A.add)
+    ts("ict", "sb", f(2), ict[:, 32:33], -0.125, A.mult)
+    ts("ict", "sb", f(3), ict[:, 32:33], -0.125, A.mult, -2.0, A.add)
+    ts("ict", "nbc", f(4), lo, -2.0, A.mult, -16384.0 * 96, A.add)
 
     o1 = T.o1
     ts("btw", "b0", o1[:, 0:12], T.btw[:], 1, A.bitwise_and)
-    ts("btw", "b1", o1[:, 12:24], T.btw[:], 1, A.arith_shift_right)
     ts("stw", "e0", o1[:, 24:36], T.stw[:], 2, A.mult)
-    copy("b1", "b1u", T.b1u[:], o1[:, 12:24])
     tt("e0 b0", "e1", o1[:, 36:48], o1[:, 24:36], o1[:, 0:12], A.add)
-    copy("stw", "stu", T.stu[:], T.stw[:])
     ts("e1", "e2", o1[:, 48:60], o1[:, 36:48], 1025, A.mult)
     ts("e2", "e3", o1[:, 24:36], o1[:, 48:60], 4, A.arith_shift_right, 1023, A.bitwise_and)
     copy("e3", "off1", T.off1[:], o1[:, 24:36])
     copy("nxrow off1", "n1r", T.n1r[:], T.nxrow[:].indirect(T.off1[:]))
     op("g", "n1r", "n1L", lambda e: e.partition_broadcast(T.n1L[:], T.n1r[0:1, :], 128))
-    fill("nxl", T.nxl[:, 1024:1032], N * TN)
-    op("g", "nxrow", "nxl", lambda e: e.partition_broadcast(T.nxl[:, 0:1024], T.nxrow[0:1, :], 128))
+    copy("nxw", "nxf", T.nxf[0:32, :], T.nxw[0:32, :])
+    turn("nxf", "nxt", T.nxt[0:32, :], T.nxf[0:32, :])
+    for b in range(2):
+        dma("y", "dnl", "nxt", "nxlin", T.nxlin[0:1, 512 * b:512 * b + 512], T.nxt[0:32, 32 * b:32 * b + 16])
+    op("g", "nxlin", "nxl", lambda e: e.partition_broadcast(T.nxl[:, 0:1024], T.nxlin[0:1, :], 128))
+    iota("nxl", T.nxl[:, 1024:1032], [[0, 8]], N * TN)
+    ts("btw", "b1", o1[:, 12:24], T.btw[:], 1, A.arith_shift_right)
+    copy("b1", "b1u", T.b1u[:], o1[:, 12:24])
     copy("ioL0 b1u", "b1L", T.b1L[:], T.ioL[:, 0:8].indirect(T.b1u[:]))
     tt("b1L kL", "kb", T.kb[:], T.b1L[:], T.kL[:, 0:V], A.add)
-    copy("kL", "aL", T.aL[:, V:208], T.kL[:, V:208])
-    fill("x1", T.x1[:], 0.0)
-    fill("x2", T.x2[:], 0.0)
-    ts("n1L lo", "ga", T.ga[:], T.n1L[:], f(0), A.is_ge)
+    ts("n1L ict", "ga", T.ga[:], T.n1L[:], lo, A.is_ge)
     ts("n1L hi", "gb", T.gb[:], T.n1L[:], f(1), A.is_ge)
-    op("v", "ga gb", "c1L", lambda e: e.tensor_tensor_scan(T.c1L[:], T.ga[:], T.gb[:], 0.0, A.add, A.subtract))
+    scan("ga gb", "c1L", T.c1L[:], T.ga[:], T.gb[:], 0.0, A.subtract)
+    copy("n1L", "a1", T.a1[:], T.n1L[:], q="s", scale=2.0)
     for k in range(2):
-        op("s", "c1L sb", "cnt1 sgx%d" % k, lambda e: e.activation(T["sg%d" % k][:, 0:V], T.c1L[:], F.Sign, bias=f(2 + k),
-                                                                 accum_out=T.cnt1[:, k:k + 1]))
-    ts("n1L", "a1", T.a1[:], T.n1L[:], 2.0, A.mult)
+        count("c1L sb", "cnt1 sgx%d" % k, T["sg%d" % k][:], T.c1L[:], f(2 + k), T.cnt1[:, k:k + 1])
     tt("a1 kb", "aL", T.aL[:, 0:V], T.a1[:], T.kb[:], A.add)
-    ts("cnt1", "nb", T.nb[:], T.cnt1[:], 8192.0, A.mult, -16384.0 * 96, A.add)
-    ts("cnt1", "i2", T.i2[:], T.cnt1[:], -0.5, A.mult, 96.0, A.add)
+    ts("ict", "nsc", f(5), lo, 2.0, A.mult, 1024.0, A.add)
+    ts("kL nsc", "aL", T.aL[:, V:208], T.kL[:, V:208], f(5), A.add)
+    ts("cnt1 nbc", "nb", T.nb[:], T.cnt1[:], 8192.0, A.mult, f(4), A.add)
     op("s", "aL nb", "ab1", lambda e: e.activation(T.ab1[:], T.aL[:], F.Abs, bias=T.nb[:, 1:2]))
     ts("aL nb", "sub0", T.sub0[:], T.aL[:], T.nb[:, 0:1], A.add)
-    ts("i2", "em", T.em[:], T.i2[:], float(V), A.is_ge, 2047.0, A.mult)
-    ts("i2", "kk", T.kk[:], T.i2[:], float(V * r), A.add)
+    ts("cnt1", "pk", T.pk[:], T.cnt1[:], -1024.0, A.mult, 2048.0 * (96 + V * r), A.add)
     op("v", "sub0", "vv", lambda e: e.tensor_reduce(T.vv[:, 0:1], T.sub0[:], AxisListType.X, A.min, apply_absolute_value=True))
-    tt("kk em", "kk2", T.pk[:], T.kk[:], T.em[:], A.max)
+    fill("x1", T.x1[:], 0.0)
     op("v", "ab1", "vv", lambda e: e.tensor_reduce(T.vv[:, 1:2], T.ab1[:], AxisListType.X, A.min))
-    ts("kk2", "pk", T.kk[:], T.pk[:], 8192.0, A.mult)
-    tt("pk vv", "x1", T.x1[:, 0:64:32], T.kk[:], T.vv[:], A.add)
+    tt("pk vv", "x1", T.x1[:, 0:64:32], T.pk[:], T.vv[:], A.add)
     turn("x1", "x1t", T.x1t[:], T.x1[:])
     for k in range(8):
         dma("y" if k % 2 else "s", "dc1", "x1t", "w1", T.w1[16 * k:16 * k + 16, :], T.x1t[0:128:32, :])
-    send("w1", "al1", lambda k: T.w1[:, 2 * k:2 * k + 2], lambda j: T.land1[:, 2 * j:2 * j + 2])
+    send("w1", "al1", lambda d: T.w1[:, 2 * d:2 * d + 2], lambda j: T.land1[:, 2 * j:2 * j + 2])
 
-    copy("c1", "odd", f(4), c(1))
-    ts("c1", "even", f(5), c(1), -1.0, A.mult, 1.0, A.add)
-    ts("ip", "c10", c(10), T.ip[:], 15, A.bitwise_and)
-    ts("ip", "c11", c(11), T.ip[:], 31, A.bitwise_and)
-    copy("c10", "q15", f(6), c(10))
-    copy("c11", "q31", f(7), c(11))
-    ts("wab q31", "wac", T.wac[:], T.wab[:], f(7), A.add)
-    ts("cw0 q15", "cw", T.cw[:], T.cw0[:], f(6), A.add)
-    ts("cw", "dw", T.dw[:], T.cw[:], float(KEYS), A.add)
+    ts("wab ict", "wac", T.wac[:], T.wab[:], q31, A.add)
     copy("n1L wac", "own", T.own[:], T.n1L[:].indirect(T.wac[:, 0:12]), q="s")
+    ts("cw0 ict", "cw", T.cw[:], T.cw0[:], q15, A.add)
+    ts("ict", "even", f(6), odd, -1.0, A.mult, 1.0, A.add)
+    ts("cw", "dw", T.dw[:], T.cw[:], float(KEYS), A.add)
+    ts("cw", "kw", fw[:, 0:12], T.cw[:, 0:12], float(V * r), A.add)
+    copy("stw", "stu", T.stu[:], T.stw[:])
     op("v", "xt", "xq xs", lambda e: e.quantize_mx(T.xq[:], T.xs[:], T.xt[:]))
     pick("xq", "xs", "stq", "sts", T.stq[:], T.sts[:], T.xq[:], T.xs[:], T.stu[:], "stu")
     turn("own", "ownt", T.ownt[:], T.own[:])
-    copy("w1", "w1i", T.w1i[:], T.w1[:, 0:14])
-    ts("w1i", "w1k", T.w1k[:], T.w1i[:], 13, A.arith_shift_right)
+    copy("w1", "w1i", T.w1i[:], T.w1[:])
+    ts("w1i", "w1k", T.w1k[:], T.w1i[:], 11, A.arith_shift_right)
     ts("w1k", "s1off", T.s1off[:], T.w1k[:], -V * r, A.add, V - 1, A.min)
     pick("stq", "sts", "p1q", "p1s", T.p1q[:], T.p1s[:], T.stq[:], T.sts[:], T.s1off[:], "s1off")
-    send("p1q", "aq1", lambda k: T.p1q[:, CAP * k:CAP * k + CAP].bitcast(dt.uint8),
+    send("p1q", "aq1", lambda d: T.p1q[:, CAP * d:CAP * d + CAP].bitcast(dt.uint8),
          lambda j: T.cq[:, V + CAP * j:V + CAP * j + CAP].bitcast(dt.uint8))
-    send("p1s", "as1", lambda k: T.p1s[:, CAP * k:CAP * k + CAP], lambda j: T.cs[:, V + CAP * j:V + CAP * j + CAP])
-    iota("bm", T.bm[:, 0:KEYS], [[0, KEYS]], 0, 0)
-    iota("ones", T.ones[:], [[0, CAND]], 1, 0)
-    deps("y", ["w1"], [])
+    send("p1s", "as1", lambda d: T.p1s[:, CAP * d:CAP * d + CAP], lambda j: T.cs[:, V + CAP * j:V + CAP * j + CAP])
+    dma("y", "dcq", "stq", "cq0", T.cq[:, 0:V].bitcast(dt.uint8), T.stq[:].bitcast(dt.uint8))
+    dma("y", "dcq", "sts", "cs0", T.cs[:, 0:V], T.sts[:])
     dma("y", "dw_", "", "wt", T.wt[:], T.w[:])
+    iota("keyL", T.keyL[:, 0:V], [[1, V]], V * r)
+    iota("infoX", T.infoL[:, CAND:CX], [[1, CAP]], KEYS + CAND + CAP * r)
+    iota("ioL", T.ioL[:, 256:KW], [[1, KW - 256]], 256)
+    iota("ones", T.ones[:], [[0, CAND]], 1)
+    iota("sT", T.sT[:, 0:KEYS], [[1, 8], [0, V]], 0)
+    iota("sT", T.sT[:, KEYS:KW], [[0, 8]], 0)
+    iota("iT", T.iT[:, KEYS:KW], [[0, 8]], 0)
     ow = T.ow
     copy("ownt", "n1w", ow[:, 0:12], T.ownt[:, 0:V:16])
     ts("n1w", "oc", ow[:, 12:24], ow[:, 0:12], 511, A.bitwise_and)
     ts("n1w", "oa", ow[:, 24:36], ow[:, 0:12], 9, A.arith_shift_right)
     ts("oc", "od", ow[:, 36:48], ow[:, 12:24], 2, A.mult)
-    ts("oa", "of", ow[:, 48:60], ow[:, 24:36], r, A.not_equal, 1024, A.mult)
+    ts("oa", "of", ow[:, 48:60], ow[:, 24:36], r, A.not_equal, 2048, A.mult)
     tt("od b1", "oe", ow[:, 60:72], ow[:, 36:48], o1[:, 12:24], A.add)
     copy("oc", "c1u0", T.c1u[:, 0:12], ow[:, 12:24])
-    ts("oe", "oe2", ow[:, 72:84], ow[:, 60:72], 1025, A.mult)
-    ts("oe2", "oe3", ow[:, 84:96], ow[:, 72:84], 4, A.arith_shift_right, 1023, A.bitwise_and)
-    tt("oe3 of", "oe4", ow[:, 36:48], ow[:, 84:96], ow[:, 48:60], A.max)
-    copy("oe4", "noff0", T.noff[:, 0:12], ow[:, 36:48])
+    tt("oe of", "og", ow[:, 72:84], ow[:, 60:72], ow[:, 48:60], A.add)
+    ts("og", "noff0", T.noff[:, 0:12], ow[:, 72:84], 1024, A.min)
     copy("nxl noff0", "n2L0", T.n2L[:, 0:V], T.nxl[:].indirect(T.noff[:, 0:12]))
-    ts("n2L0 lo", "g2a0", T.g2a[:, 0:V], T.n2L[:, 0:V], f(0), A.is_ge)
+    ts("n2L0 ict", "g2a0", T.g2a[:, 0:V], T.n2L[:, 0:V], lo, A.is_ge)
     ts("n2L0 hi", "g2b0", T.g2b[:, 0:V], T.n2L[:, 0:V], f(1), A.is_ge)
-    op("v", "g2a0 g2b0", "c2L0", lambda e: e.tensor_tensor_scan(T.c2L[:, 0:V], T.g2a[:, 0:V], T.g2b[:, 0:V], 0.0, A.add, A.subtract))
+    scan("g2a0 g2b0", "c2L0", T.c2L[:, 0:V], T.g2a[:, 0:V], T.g2b[:, 0:V], 0.0, A.subtract)
     for k in range(2):
-        op("s", "c2L0 sb", "cnt2o sgy%d" % k, lambda e: e.activation(T["sg%d" % (2 + k)][:, 0:V], T.c2L[:, 0:V], F.Sign, bias=f(2 + k),
-                                                                   accum_out=T.cnt2[:, k:k + 1]))
-    op("s", "n2L0", "inf00", lambda e: e.activation(T.inf0[:, 0:V], T.n2L[:, 0:V], F.Copy, scale=2048.0))
-    pick("xq", "xs", "cq0", "cs0", T.cq[:, 0:V], T.cs[:, 0:V], T.xq[:], T.xs[:], T.stu[:], "stu")
-    ts("cnt2o", "cnt2h", T.cnt2[:, 2:4], T.cnt2[:, 0:2], -0.5, A.mult, CAND / 2.0, A.add)
-    pick("xq", "xs", "cq1", "cs1", T.cq[:, CAND:CAND + V], T.cs[:, CAND:CAND + V], T.xq[:], T.xs[:], T.c1u[:, 0:12], "c1u0")
-    ts("ioL0", "keyL", T.keyL[:, 0:V], T.ioL[:, 0:V], float(V * r), A.add)
-    ts("cw", "kw", T.fw[:, 0:12], T.cw[:, 0:12], float(V * r), A.add)
-    for k in range(1, 3):
-        ts("ioL0", "ioL", T.ioL[:, 512 * k:512 * k + 512], T.ioL[:, 0:512], 512.0 * k, A.add)
-    tt("inf00 keyL", "infoL", T.infoL[:, 0:V], T.inf0[:, 0:V], T.keyL[:, 0:V], A.add)
-    fill("infoL", T.infoL[:, CAND:424], 2047.0)
+        count("c2L0 sb", "cnt2o sgy%d" % k, T["sg%d" % (2 + k)][:, 0:V], T.c2L[:, 0:V], f(2 + k), T.cnt2[:, k:k + 1])
+    copy("n2L0", "inf00", T.inf0[:, 0:V], T.n2L[:, 0:V], q="s", scale=4096.0)
+    fill("x2", T.x2[:], 0.0)
 
     wrote["land1"] = [arrivals("al1")]
     wrote["cqa"] = [arrivals("aq1")]
     wrote["csa"] = [arrivals("as1")]
     l1 = T.l1
     copy("land1", "l1", l1[:, 0:14], T.land1[:])
-    ts("l1", "la", l1[:, 14:28], l1[:, 0:14], 1023, A.bitwise_and)
-    ts("l1", "lk", l1[:, 28:42], l1[:, 0:14], 13, A.arith_shift_right)
-    ts("la", "lb", l1[:, 42:56], l1[:, 14:28], 1025, A.mult)
-    ts("lk", "li", l1[:, 56:70], l1[:, 28:42], KEYS, A.is_ge, 1024, A.mult)
-    ts("lb", "lc", l1[:, 70:84], l1[:, 42:56], 4, A.arith_shift_right, 1023, A.bitwise_and)
-    tt("lc li", "ld", l1[:, 84:98], l1[:, 70:84], l1[:, 56:70], A.max)
-    copy("ld", "noff1", T.noff[:, 12:26], l1[:, 84:98])
+    ts("l1", "la", l1[:, 14:28], l1[:, 0:14], 2047, A.bitwise_and)
+    copy("la", "noff1", T.noff[:, 12:26], l1[:, 14:28])
     copy("nxl noff1", "n2L1", T.n2L[:, V:CAND], T.nxl[:].indirect(T.noff[:, 12:26]))
-    ts("n2L1 lo", "g2a1", T.g2a[:, V:CAND], T.n2L[:, V:CAND], f(0), A.is_ge)
+    ts("n2L1 ict", "g2a1", T.g2a[:, V:CAND], T.n2L[:, V:CAND], lo, A.is_ge)
     ts("n2L1 hi", "g2b1", T.g2b[:, V:CAND], T.n2L[:, V:CAND], f(1), A.is_ge)
-    op("v", "g2a1 g2b1 c2L0", "c2L1", lambda e: e.tensor_tensor_scan(T.c2L[:, V:CAND], T.g2a[:, V:CAND], T.g2b[:, V:CAND],
-                                                                  T.c2L[:, V - 1:V], A.add, A.subtract))
+    scan("g2a1 g2b1 c2L0", "c2L1", T.c2L[:, V:CAND], T.g2a[:, V:CAND], T.g2b[:, V:CAND], T.c2L[:, V - 1:V], A.subtract)
+    ts("ioL0 c2L1", "c2L2", T.c2L[:, CAND:CX], T.ioL[:, 1:1 + CAP], T.c2L[:, CAND - 1:CAND], A.add)
     for k in range(2):
-        op("s", "c2L1 sb", "cnt2a sgz%d" % k, lambda e: e.activation(T["sg%d" % (2 + k)][:, V:CAND], T.c2L[:, V:CAND], F.Sign, bias=f(2 + k),
-                                                                   accum_out=T.cnt2[:, 4 + k:5 + k]))
-    ts("l1", "le", l1[:, 98:112], l1[:, 0:14], 1, A.arith_shift_right, 511, A.bitwise_and)
-    ts("lk", "ku1", T.ku1[:], l1[:, 28:42], KEYS - 1, A.min)
-    copy("le", "c1u1", T.c1u[:, 12:26], l1[:, 98:112])
+        count("c2L1 c2L2 sb", "cnt2a sgz%d" % k, T["sg%d" % (2 + k)][:, V:CX], T.c2L[:, V:CX], f(2 + k), T.cnt2[:, 4 + k:5 + k])
+    ts("cnt2o", "cnt2h", T.cnt2[:, 2:4], T.cnt2[:, 0:2], -0.5, A.mult, CX / 2.0, A.add)
+    ts("l1", "lk", l1[:, 28:42], l1[:, 0:14], 11, A.arith_shift_right)
+    ts("l1", "le", l1[:, 42:56], l1[:, 0:14], 1, A.arith_shift_right, 511, A.bitwise_and)
+    copy("lk", "ku1", T.ku1[:], l1[:, 28:42])
     ts("cnt2a", "cnt2b", T.cnt2[:, 6:8], T.cnt2[:, 4:6], -0.5, A.mult)
     tt("cnt2b cnt2h", "x2", T.x2[:, 0:64:32], T.cnt2[:, 6:8], T.cnt2[:, 2:4], A.add)
     turn("x2", "x2t", T.x2t[:], T.x2[:])
     for k in range(8):
         dma("y" if k % 2 else "s", "dc2", "x2t", "w2", T.w2[16 * k:16 * k + 16, :], T.x2t[0:128:32, :])
-    pick("xq", "xs", "cq2", "cs2", T.cq[:, CAND + V:2 * CAND], T.cs[:, CAND + V:2 * CAND], T.xq[:], T.xs[:], T.c1u[:, 12:26], "c1u1")
+    copy("n2L1", "inf01", T.inf0[:, V:CAND], T.n2L[:, V:CAND], q="s", scale=4096.0)
     copy("ioL0 ioL ku1", "keyL1", T.keyL[:, V:CAND], T.ioL[:].indirect(T.ku1[:]), q="s")
-    op("s", "n2L1", "inf01", lambda e: e.activation(T.inf0[:, V:CAND], T.n2L[:, V:CAND], F.Copy, scale=2048.0))
-    copy("n2L0 n2L1 wac", "n2g", T.n2g[:], T.n2L[:].indirect(T.wac[:, 0:26]), q="s")
-    tt("inf01 keyL1", "infoL", T.infoL[:, V:CAND], T.inf0[:, V:CAND], T.keyL[:, V:CAND], A.add)
-    ts("w2", "o2off", T.o2off[:, 0:28:2], T.w2[:, 0:14], CAND - 1.0, A.min)
-    ts("w2", "o2off", T.o2off[:, 1:28:2], T.w2[:, 0:14], CAND - 1.0, A.min, float(CAND), A.add)
-    pick("cq0 cq1 cq2 cqa", "cs0 cs1 cs2 csa", "p2q", "p2s", T.p2q[:], T.p2s[:], T.cq[:], T.cs[:], T.o2off[:], "o2off")
-    send("p2q", "aq2", lambda k: T.p2q[:, 64 * k:64 * k + 64].bitcast(dt.uint8),
+    tt("inf00 keyL", "info0", T.infoL[:, 0:V], T.inf0[:, 0:V], T.keyL[:, 0:V], A.add)
+    copy("le", "c1u1", T.c1u[:, 12:26], l1[:, 42:56])
+    tt("inf01 keyL1", "info1", T.infoL[:, V:CAND], T.inf0[:, V:CAND], T.keyL[:, V:CAND], A.add)
+    pick("xq", "xs", "cq1", "cs1", T.cq[:, CAND:2 * CAND], T.cs[:, CAND:2 * CAND], T.xq[:], T.xs[:], T.c1u[:], "c1u0 c1u1")
+    copy("w2", "w2u", T.w2u[:], T.w2[:])
+    copy("info0 info1 infoX w2u", "ig", T.ig[:], T.infoL[:].indirect(T.w2u[:]))
+    copy("ig wac", "ig2", T.ig2[:], T.ig[:].indirect(T.wac[:, 0:16]))
+    turn("ig2", "igt", T.igt[:], T.ig2[:])
+    copy("igt", "l2s", T.l2s[:], T.igt[:, 0:256:16])
+    send("l2s", "al2", lambda d: T.l2s[:, 2 * d:2 * d + 2], lambda j: T.land2[:, 2 * j:2 * j + 2])
+    ts("w2", "o2off", T.o2off[:, 0:32:2], T.w2[:], CAND - 1.0, A.min)
+    ts("w2", "o2off", T.o2off[:, 1:32:2], T.w2[:], CAND - 1.0, A.min, float(CAND), A.add)
+    pick("cq0 cq1 cqa", "cs0 cs1 csa", "p2q", "p2s", T.p2q[:], T.p2s[:], T.cq[:], T.cs[:], T.o2off[:], "o2off")
+    send("p2q", "aq2", lambda d: T.p2q[:, 64 * d:64 * d + 64].bitcast(dt.uint8),
          lambda j: T.eq[:, 64 * j:64 * j + 64].bitcast(dt.uint8))
-    send("p2s", "as2", lambda k: T.p2s[:, 64 * k:64 * k + 64], lambda j: T.es[:, 64 * j:64 * j + 64])
-    xx = T.xx
-    ts("w2 even", "xa", xx[:, 0:7], T.w2[:, 0:14:2], f(5), A.mult)
-    ts("w2 odd", "xb", xx[:, 8:15], T.w2[:, 1:14:2], f(4), A.mult)
-    tt("xa xb", "xc", xx[:, 16:23], xx[:, 0:7], xx[:, 8:15], A.add)
-    copy("xc", "wau", T.wau[:, 0:14:2], xx[:, 16:23])
-    copy("xc", "wau", T.wau[:, 1:14:2], xx[:, 16:23])
-    copy("infoL wau", "ig", T.ig[:], T.infoL[:].indirect(T.wau[:]))
-    turn("ig", "igt", T.igt[:], T.ig[:])
-    copy("igt", "l2s", T.l2s[:], T.igt[:, 0:ARR:16])
-    send("l2s", "al2", lambda k: T.l2s[:, 2 * k:2 * k + 2], lambda j: T.land2[:, 2 * j:2 * j + 2])
-    iota("yx", T.yx[:], [[32, 14], [1, 16]], CAND, 0)
-    iota("yx2a", T.yx2[:, 0:CAND], [[2048, CAND]], 256, 0)
-    iota("pp", T.pp[:, KEYS:KEYS + ALL], [[1, ALL]], M + 1, 0)
-    iota("inv", T.inv[:, 0:M], [[0, M]], YZ * 2048 + 256 - V - 1, 0)
+    send("p2s", "as2", lambda d: T.p2s[:, 64 * d:64 * d + 64], lambda j: T.es[:, 64 * j:64 * j + 64])
+    iota("pp", T.pp[:, KEYS:KEYS + TAIL], [[1, TAIL]], M + 1)
+    iota("yx", T.yx[:, 0:CAND], [[1, CAND]], 0)
+    iota("yx", T.yx[:, CAND:ALL], [[32, 14], [1, 16]], CAND)
+    iota("inv", T.inv[:, 0:M], [[0, M]], YZ)
+    iota("iT", T.iT[:, 0:KEYS], [[0, 8], [1, V]], 0)
+    for o in range(2):
+        iota("ybz%d" % o, T["yb%d" % o][:, YZ:YZ + 8], [[0, 8]], 0)
+    iota("sW", T.sW[:, 0:V], [[0, V]], r)
+    iota("iW", T.iW[:, 0:V], [[1, V]], 0)
+    iota("sW", T.sW[:, YZ:YZ + 8], [[0, 8]], -1)
+    iota("iW", T.iW[:, YZ:YZ + 8], [[0, 8]], -1)
 
+    n2w, xx = T.n2w, T.xx
+    copy("n2L0 n2L1 wac", "n2g", T.n2g[:], T.n2L[:].indirect(T.wac[:, 0:26]), q="s")
+    copy("ioL0 ioL", "bm", T.bm[:, 0:KEYS], T.ioL[:, 0:KEYS], q="s", scale=0.0)
+    copy("lk", "kw", fw[:, 12:26], l1[:, 28:42])
     turn("n2g", "n2t", T.n2t[:], T.n2g[:])
-    n2w, fw = T.n2w, T.fw
     copy("n2t", "n2w", n2w[:, 0:26], T.n2t[:, 0:CAND:16])
-    ts("lk", "kw", fw[:, 12:26], l1[:, 28:42], KEYS - 1, A.min)
     ts("n2w", "n2e", n2w[:, 52:78], n2w[:, 0:26], 9, A.arith_shift_right)
     ts("n2w", "n2c", n2w[:, 26:52], n2w[:, 0:26], 511, A.bitwise_and)
-    ts("n2e", "bad", fw[:, 40:66], n2w[:, 52:78], r, A.not_equal)
+    ts("n2e", "bad", fw[:, 26:52], n2w[:, 52:78], r, A.not_equal)
     copy("n2c", "c2u", T.c2u[:], n2w[:, 26:52])
-    tt("bad dw", "badd", fw[:, 80:106], fw[:, 40:66], T.dw[:, 0:26], A.mult)
+    tt("bad dw", "badd", fw[:, 52:78], fw[:, 26:52], T.dw[:, 0:26], A.mult)
     pick("xq", "xs", "n2q", "n2s", T.n2q[:], T.n2s[:], T.xq[:], T.xs[:], T.c2u[:], "c2u")
-    tt("kw badd", "ko0", T.ko[:, 0:26], fw[:, 0:26], fw[:, 80:106], A.max)
+    tt("kw badd", "ko", T.ko[:], fw[:, 0:26], fw[:, 52:78], A.max)
     op("v", "wt", "wq0 ws0", lambda e: e.quantize_mx(T.wq[:, 0:384], T.ws[:, 0:384], T.wt[:, 0:1536]))
-    copy("ko0", "kou0", T.kou[:, 0:26], T.ko[:, 0:26])
+    copy("ko", "kou0", T.kou[:, 0:26], T.ko[:])
     op("v", "wt", "wq1 ws1", lambda e: e.quantize_mx(T.wq[:, 384:768], T.ws[:, 384:768], T.wt[:, 1536:3072]))
     op("v", "kou0 ones", "bm", lambda e: e.tensor_copy(T.bm[:].indirect(T.kou[:, 0:26]), T.ones[:]))
+    ts("ko even", "qa", xx[:, 0:13], T.ko[:, 0:26:2], f(6), A.mult)
+    ts("ko ict", "qb", xx[:, 13:26], T.ko[:, 1:26:2], odd, A.mult)
+    tt("qa qb", "qc", xx[:, 26:39], xx[:, 0:13], xx[:, 13:26], A.add)
+    copy("qc", "pwa", T.pwa[:, 0:26:2], xx[:, 26:39])
+    copy("qc", "pwa", T.pwa[:, 1:26:2], xx[:, 26:39])
 
     W = lambda k, o: (T.wq[:, 128 * (2 * k + o):128 * (2 * k + o) + 128], T.ws[:, 128 * (2 * k + o):128 * (2 * k + o) + 128])
 
@@ -375,68 +374,56 @@ def rank_program(g, core, T, topo):
 
     for o in range(2):
         mm("cq0 cqa cs0 csa", "psS%d" % o, o, CAND, 0, o, T.cq[:, 0:CAND], T.cs[:, 0:CAND], True, False)
-        mm("cq1 cq2 cs1 cs2", "psS%d" % o, o, CAND, 1, o, T.cq[:, CAND:2 * CAND], T.cs[:, CAND:2 * CAND], False, False)
+        mm("cq1 cs1", "psS%d" % o, o, CAND, 1, o, T.cq[:, CAND:2 * CAND], T.cs[:, CAND:2 * CAND], False, False)
         mm("n2q n2s", "psS%d" % o, o, CAND, 2, o, T.n2q[:], T.n2s[:], False, True)
-    tt("yx2a keyL keyL1", "tk0", T.tk[:, 0:CAND], T.yx2[:, 0:CAND], T.keyL[:, 0:CAND], A.add)
-    ts("yx", "yx2b", T.yx2[:, CAND:ALL], T.yx[:], 2048.0, A.mult, 256.0, A.add)
-    for o in range(2):
-        fill("yb%d" % o, T["yb%d" % o][:, YZ:YZ + 8], 0.0)
 
     wrote["land2"] = [arrivals("al2")]
     wrote["eqa"] = [arrivals("aq2")]
     wrote["esa"] = [arrivals("as2")]
     l2 = T.l2i
     copy("land2", "m0", l2[:, 0:14], T.land2[:])
-    ts("m0", "m1", l2[:, 14:28], l2[:, 0:14], 2047, A.bitwise_and)
-    ts("m0", "m2", l2[:, 28:42], l2[:, 0:14], 11, A.arith_shift_right, 511, A.bitwise_and)
-    ts("m1", "m3", fw[:, 106:120], l2[:, 14:28], KEYS, A.is_ge)
-    ts("m1", "m4", fw[:, 120:134], l2[:, 14:28], KEYS - 1, A.min)
-    ts("m1", "ku2", T.ku2[:], l2[:, 14:28], KEYS - 1, A.min)
-    tt("m3 dw", "m5", fw[:, 134:148], fw[:, 106:120], T.dw[:, 26:40], A.mult)
-    copy("m2", "c2ua", T.c2ua[:, 0:28:2], l2[:, 28:42])
-    copy("m2", "c2ua", T.c2ua[:, 1:28:2], l2[:, 28:42])
-    tt("m4 m5", "ko1", T.ko[:, 26:40], fw[:, 120:134], fw[:, 134:148], A.max)
-    copy("ko1", "kou1", T.kou[:, 26:40], T.ko[:, 26:40])
+    ts("m0", "m1", l2[:, 14:28], l2[:, 0:14], 4095, A.bitwise_and)
+    copy("m1", "kou1", T.kou[:, 26:40], l2[:, 14:28])
     op("v", "kou1 ones", "bm", lambda e: e.tensor_copy(T.bm[:].indirect(T.kou[:, 26:40]), T.ones[:, 0:ARR]))
-    copy("ioL0 ioL ku2", "keyL2", T.keyL[:, CAND:ALL], T.ioL[:].indirect(T.ku2[:]), q="s")
+    ts("m0", "m2", l2[:, 28:42], l2[:, 0:14], 12, A.arith_shift_right, 511, A.bitwise_and)
+    ts("m1 even", "qd", xx[:, 39:46], l2[:, 14:28:2], f(6), A.mult)
+    ts("m1 ict", "qe", xx[:, 46:53], l2[:, 15:28:2], odd, A.mult)
+    scan("bm", "pp", T.pp[:, 0:KEYS], T.bm[:, 0:KEYS], T.bm[:, 0:KEYS], 0.0, A.max)
+    tt("qd qe", "qf", xx[:, 53:60], xx[:, 39:46], xx[:, 46:53], A.add)
+    copy("m2", "c2ua", T.c2ua[:, 0:28:2], l2[:, 28:42])
+    copy("qf", "pwb", T.pwa[:, 26:40:2], xx[:, 53:60])
+    copy("qf", "pwb", T.pwa[:, 27:40:2], xx[:, 53:60])
+    copy("m2", "c2ua", T.c2ua[:, 1:28:2], l2[:, 28:42])
+    copy("pp pwa", "pg0", T.pg[:, 0:320], T.pp[:].indirect(T.pwa[:, 0:20]))
+    copy("pp pwa pwb", "pg1", T.pg[:, 320:ALL], T.pp[:].indirect(T.pwa[:, 20:40]), q="s")
+    turn("pg0", "pt0", T.pt[:, 0:320], T.pg[:, 0:320])
+    ts("m1", "ku2", T.ku2[:, 0:28:2], l2[:, 14:28], KEYS - 1, A.min)
+    ts("m1", "ku2", T.ku2[:, 1:28:2], l2[:, 14:28], KEYS - 1, A.min)
+    turn("pg1", "pt1", T.pt[:, 320:ALL], T.pg[:, 320:ALL])
+    ts("pt0 pt1", "plu", T.plu[:], T.pt[:, 0:ALL:16], -1.0, A.add)
     pick("xq", "xs", "fq", "fs", T.fq[:], T.fs[:], T.xq[:], T.xs[:], T.c2ua[:, 0:27], "c2ua")
-    for o in range(2):
-        copy("psS%d" % o, "yb%d" % o, T["yb%d" % o][:, 0:CAND], T.ps[:, 512 * o:512 * o + CAND], q="s")
-    for o in range(2):
-        mm("fq fs", "psA%d" % o, 2 + o, SPREAD, 2, o, T.fq[:], T.fs[:], True, False)
-    ts("ko0 ko1 even", "q0", fw[:, 0:20], T.ko[:, 0:40:2], f(5), A.mult)
-    ts("ko0 ko1 odd", "q1", fw[:, 20:40], T.ko[:, 1:40:2], f(4), A.mult)
-    op("v", "bm", "pp", lambda e: e.tensor_tensor_scan(T.pp[:, 0:KEYS], T.bm[:, 0:KEYS], T.bm[:, 0:KEYS], 0.0, A.add, A.max))
-    tt("q0 q1", "q2", fw[:, 40:60], fw[:, 0:20], fw[:, 20:40], A.add)
-    copy("q2", "pwa", T.pwa[:, 0:40:2], fw[:, 40:60])
-    copy("q2", "pwa", T.pwa[:, 1:40:2], fw[:, 40:60])
-    copy("pp pwa", "pg", T.pg[:], T.pp[:].indirect(T.pwa[:]))
-    turn("pg", "pt", T.pt[:], T.pg[:])
-    tt("yx2b keyL2", "tk1", T.tk[:, CAND:ALL], T.yx2[:, CAND:ALL], T.keyL[:, CAND:ALL], A.add)
-    ts("pt", "plu", T.plu[:], T.pt[:, 0:ALL:16], -1.0, A.add)
-    op("v", "plu tk0 tk1", "inv", lambda e: e.tensor_copy(T.inv[:].indirect(T.plu[:]), T.tk[:]))
+    op("v", "plu yx", "inv", lambda e: e.tensor_copy(T.inv[:].indirect(T.plu[:]), T.yx[:]))
     copy("inv wac", "ivg", T.ivg[:], T.inv[:, 0:M].indirect(T.wac[:, 0:18]))
     turn("ivg", "ivt", T.ivt[:], T.ivg[:])
-    copy("ivt", "ivi", T.ivi[:, 0:18], T.ivt[:, 0:M:16])
-    ts("ivi", "ivj", T.ivi[:, 18:36], T.ivi[:, 0:18], 11, A.arith_shift_right)
-    copy("ivj", "ylu", T.ylu[:], T.ivi[:, 18:36])
+    copy("ivt", "ylu", T.ylu[:], T.ivt[:, 0:M:16])
+    for o in range(2):
+        mm("fq fs", "psA%d" % o, 2 + o, SPREAD, 2, o, T.fq[:], T.fs[:], True, False)
+    for o in range(2):
+        copy("psS%d" % o, "yb%d" % o, T["yb%d" % o][:, 0:CAND], T.ps[:, 512 * o:512 * o + CAND], q="s")
+    for t_, w_ in (("sT", "sW"), ("iT", "iW")):
+        copy(t_ + " ku1", w_, T[w_][:, V:CAND], T[t_][:].indirect(T.ku1[:]), q="s")
+        copy(t_ + " ku2", w_, T[w_][:, CAND:YZ], T[t_][:].indirect(T.ku2[:, 0:27]), q="s")
     for o in range(2):
         mm("eqa esa", "psA%d" % o, 2 + o, SPREAD, 0, o, T.eq[:, 0:SPREAD], T.es[:, 0:SPREAD], False, False)
         mm("eqa esa", "psA%d" % o, 2 + o, SPREAD, 1, o, T.eq[:, 16:16 + SPREAD], T.es[:, 16:16 + SPREAD], False, True)
-    ik, fd = T.idk, T.idf
-    I = lambda j: ik[:, M * j:M * j + M]
-    D = lambda j: fd[:, M * j:M * j + M]
-    ts("inv", "i1", I(0), T.inv[:, 0:M], 2047, A.bitwise_and)
-    ts("i1", "i2x", I(1), I(0), 1.0 / V, A.mult, -255.5 / V - 0.5, A.add)
-    ts("i2x", "d0", D(0), I(1), -1.0, A.max)
-    ts("d0", "d1", D(1), D(0), -float(V), A.mult, -256.0, A.add)
-    tt("d1 i1", "d2", D(2), D(1), I(0), A.add)
-    dma("y", "did", "d0", "id0", T["id"][0:1, :], fd[0:1, 0:M])
-    dma("y", "did", "d2", "id1", T["id"][1:2, :], fd[0:1, 2 * M:3 * M])
-    copy("psA0", "yb0", T.yb0[:, CAND:YZ], T.ps[:, 1024:1024 + SPREAD])
+    copy("psA0", "yb0", T.yb0[:, CAND:YZ], T.ps[:, 1024:1024 + SPREAD], q="s")
     copy("psA1", "yb1", T.yb1[:, CAND:YZ], T.ps[:, 1536:1536 + SPREAD], q="s")
-    copy("yb0 ylu", "yo0", T.yo0[:], T.yb0[:].indirect(T.ylu[:]))
-    copy("yb1 ylu", "yo1", T.yo1[:], T.yb1[:].indirect(T.ylu[:]), q="s")
+    copy("yb0 ybz0 ylu", "yo0", T.yo0[:], T.yb0[:].indirect(T.ylu[:]))
     dma("y", "dy0", "yo0", "y0", T.y[:, 0:M], T.yo0[:])
+    copy("yb1 ybz1 ylu", "yo1", T.yo1[:], T.yb1[:].indirect(T.ylu[:]), q="s")
     dma("s", "dy1", "yo1", "y1", T.y[:, M:2 * M], T.yo1[:])
+    copy("sW ylu", "ids", T.ids[:], T.sW[:].indirect(T.ylu[:]))
+    dma("y", "did", "ids", "id0", T["id"][0:1, :], T.ids[0:1, :])
+    copy("iW ylu", "idi", T.idi[:], T.iW[:].indirect(T.ylu[:]), q="s")
+    dma("s", "did2", "idi", "id1", T["id"][1:2, :], T.idi[0:1, :])
     await_("g", [(s, None) for s in total])

from concourse.bass import DstId, RemoteDMATransfer
from concourse.mybir import dt, AluOpType as A, AxisListType, ActivationFunctionType as F

N = 8
TN, V, M, KEYS = 512, 192, 288, 1536
CAP = 32
ARR = (N - 1) * CAP
CAND = V + ARR
CX = CAND + CAP
ALL = CAND + ARR
TAIL = CAND + N * CAP
SPREAD = 2 * ARR - 16
YZ = CAND + SPREAD
KW = 1544
X4 = "float8_e4m3fn_x4"


def _sb(n, d="float32"):
    return ("sbuf", [128, n], d)


SCRATCH = {
    "stw": _sb(12, "int32"), "btw": _sb(12, "int32"), "nxrow": _sb(1024, "int32"), "nxw": _sb(64, "int32"), "nxf": _sb(64),
    "nxt": _sb(64), "nxlin": _sb(1024), "nxl": _sb(1032), "xt": _sb(2048, "bfloat16"), "wt": _sb(3072, "bfloat16"),
    "ic": _sb(160), "ict": _sb(160), "cf": _sb(16), "ioL": _sb(KW), "kL": _sb(208), "wab": _sb(40, "int32"), "cw0": _sb(40),
    "wac": _sb(40, "uint16"), "cw": _sb(40), "dw": _sb(40), "yx": _sb(ALL), "sT": _sb(KW), "iT": _sb(KW),
    "o1": _sb(64, "int32"), "off1": _sb(12, "uint16"), "b1u": _sb(12, "uint16"), "stu": _sb(12, "uint16"),
    "n1r": _sb(V), "n1L": _sb(V), "b1L": _sb(V), "kb": _sb(V), "a1": _sb(V), "aL": _sb(208),
    "ga": _sb(V), "gb": _sb(V), "c1L": _sb(V), "sg0": _sb(V), "sg1": _sb(V), "sg2": _sb(CX), "sg3": _sb(CX),
    "cnt1": _sb(2), "nb": _sb(2), "sub0": _sb(208), "ab1": _sb(208), "vv": _sb(2), "pk": _sb(2),
    "x1": _sb(64), "x1t": _sb(64), "w1": _sb(16), "w1i": _sb(16, "int32"), "w1k": _sb(16, "int32"),
    "s1off": _sb(16, "uint16"), "land1": _sb(14),
    "own": _sb(V), "ownt": _sb(V), "ow": _sb(96, "int32"), "noff": _sb(26, "uint16"), "c1u": _sb(26, "uint16"),
    "n2L": _sb(CAND), "g2a": _sb(CAND), "g2b": _sb(CAND), "c2L": _sb(CX), "l1": _sb(64, "int32"),
    "cnt2": _sb(8), "x2": _sb(64), "x2t": _sb(64), "w2": _sb(16), "o2off": _sb(32, "uint16"), "w2u": _sb(16, "uint16"),
    "ku1": _sb(14, "uint16"), "keyL": _sb(CAND), "inf0": _sb(CAND), "infoL": _sb(CX),
    "ig": _sb(256), "ig2": _sb(256), "igt": _sb(256), "l2s": _sb(16), "land2": _sb(14),
    "n2g": _sb(CAND), "n2t": _sb(CAND), "n2w": _sb(80, "int32"), "c2u": _sb(26, "uint16"), "fw": _sb(120), "xx": _sb(60),
    "ko": _sb(26), "kou": _sb(40, "uint16"), "pwa": _sb(40, "uint16"), "ones": _sb(CAND), "bm": _sb(KEYS + TAIL), "pp": _sb(KEYS + TAIL),
    "l2i": _sb(64, "int32"), "c2ua": _sb(28, "uint16"), "ku2": _sb(28, "uint16"), "sW": _sb(YZ + 8), "iW": _sb(YZ + 8),
    "pg": _sb(ALL), "pt": _sb(ALL), "plu": _sb(40, "uint16"), "inv": _sb(M + TAIL),
    "ivg": _sb(M), "ivt": _sb(M), "ylu": _sb(18, "uint16"), "ids": _sb(M), "idi": _sb(M),
    "xq": _sb(TN, X4), "xs": _sb(TN, "uint8"), "wq": _sb(768, X4), "ws": _sb(768, "uint8"),
    "stq": _sb(V, X4), "sts": _sb(V, "uint8"), "p1q": _sb(256, X4), "p1s": _sb(256, "uint8"),
    "cq": _sb(2 * CAND, X4), "cs": _sb(2 * CAND, "uint8"), "n2q": _sb(CAND, X4), "n2s": _sb(CAND, "uint8"),
    "p2q": _sb(512, X4), "p2s": _sb(512, "uint8"), "eq": _sb(2 * ARR, X4), "es": _sb(2 * ARR, "uint8"),
    "fq": _sb(SPREAD, X4), "fs": _sb(SPREAD, "uint8"),
    "yb0": _sb(YZ + 8), "yb1": _sb(YZ + 8), "yo0": _sb(M), "yo1": _sb(M),
    "ps": ("psum", [128, 2048], "float32"),
}
SEMAPHORES = ["cv", "cs_", "ct", "cg", "dst", "dbt", "dnx", "dnw", "dnl", "dx", "dw_", "dcq", "dc1", "dc2", "dy0", "dy1", "did",
              "did2", "sent", "al1", "aq1", "as1", "al2", "aq2", "as2"]


def _split(core, others, topo):
    own = topo.cores_of(core)
    far = [c for c in others if c not in own]
    near = [c for c in others if c in own]
    out, taken = {}, []
    for part in (far, near):
        if not part:
            continue
        free = [e for e in topo.engines(core, part[0]) if e not in taken]
        k = 1
        while 2 * k * len(part) <= len(free):
            k *= 2
        for j, c in enumerate(part):
            out[c] = free[j * k:(j + 1) * k]
            taken += out[c]
    return out


def rank_program(g, core, T, topo):
    r = T.rank_of(core)
    if r is None:
        return
    sem = T.sem
    queues = {"v": (g.vector, "cv"), "s": (g.scalar, "cs_"), "t": (g.tensor, "ct"), "g": (g, "cg"), "y": (g.sync, None)}
    total, seen = {}, {q: {} for q in queues}
    wrote, read = {}, {}

    def await_(q, toks):
        eng, need = queues[q][0], {}
        for s, val in toks:
            val = total[s] if val is None else val
            need[s] = max(need.get(s, 0), val)
        for s in need:
            if seen[q].get(s, 0) < need[s]:
                eng.wait_ge(sem[s], need[s])
                seen[q][s] = need[s]

    def deps(q, r_, w_, own=None):
        mine = (queues[q][1], own)
        toks = []
        for k in r_:
            toks += wrote.get(k, [])
        for k in w_:
            toks += [t for t in wrote.get(k, []) + read.get(k, []) if t[0] not in mine]
        await_(q, toks)

    def note(tok, r_, w_):
        for k in r_:
            read.setdefault(k, []).append(tok)
        for k in w_:
            wrote.setdefault(k, []).append(tok)

    def op(q, r_, w_, fn):
        r_, w_ = r_.split(), w_.split()
        deps(q, r_, w_)
        s = queues[q][1]
        total[s] = total.get(s, 0) + 1
        fn(queues[q][0]).then_inc(sem[s], 1)
        note((s, total[s]), r_, w_)

    def dma(q, s, r_, w_, out, in_):
        r_, w_ = r_.split(), w_.split()
        deps(q, r_, w_, s)
        total[s] = total.get(s, 0) + 16
        queues[q][0].dma_start(out, in_).then_inc(sem[s], 16)
        note((s, None), r_, w_)

    def copy(r_, w_, out, in_, q="v", scale=1.0):
        if q == "s":
            op("s", r_, w_, (lambda e: e.activation(out, in_, F.Copy)) if scale == 1.0 else
               (lambda e: e.activation(out, in_, F.Copy, scale=scale)))
        else:
            op(q, r_, w_, lambda e: e.tensor_copy(out, in_))

    def ts(r_, w_, out, in0, s1, o0, s2=None, o1=None):
        if o1 is None:
            op("v", r_, w_, lambda e: e.tensor_scalar(out, in0, s1, None, o0))
        else:
            op("v", r_, w_, lambda e: e.tensor_scalar(out, in0, s1, s2, o0, o1))

    def tt(r_, w_, out, a, b, o):
        op("v", r_, w_, lambda e: e.tensor_tensor(out, a, b, o))

    def fill(w_, ap, c):
        op("v", "", w_, lambda e: e.memset(ap, c))

    def turn(r_, w_, out, in_):
        op("v", r_, w_, lambda e: e.transpose(out, in_))

    def iota(w_, ap, pat, base, mult=0):
        op("g", "", w_, lambda e: e.iota(ap, pat, base, mult, allow_small_or_imprecise_dtypes=True))

    def count(r_, w_, out, in_, bias, acc):
        op("s", r_, w_, lambda e: e.activation(out, in_, F.Sign, bias=bias, accum_out=acc))

    def scan(r_, w_, out, a, b, init, o1):
        op("v", r_, w_, lambda e: e.tensor_tensor_scan(out, a, b, init, A.add, o1))

    def pick(deps_q, deps_s, w_q, w_s, oq, os_, iq, is_, off, off_key):
        copy(deps_q + " " + off_key, w_q, oq.bitcast(dt.uint32), iq.bitcast(dt.uint32).indirect(off))
        copy(deps_s + " " + off_key, w_s, os_, is_.indirect(off), q="s")

    others = [c for c in T.cores if c != core]
    engines = _split(core, others, topo)

    def arrivals(s):
        n = sum(len(_split(c, [b for b in T.cores if b != c], topo)[core]) for c in others)
        total[s] = n
        return (s, n)

    def send(r_, s, src, dst):
        deps("g", r_.split(), [])
        tr = []
        for c in others:
            d = T.rank_of(c)
            rid, pid = topo.addr(c)[:2]
            m = 0
            for e in engines[c]:
                m |= 1 << e
            tr.append(RemoteDMATransfer(dst_ids=[DstId(rid=rid, pnc=pid)], dma_engine_mask=m, remote_sem=sem[s],
                                        src=src(d), dst=dst(r - (r > d))))
            total["sent"] = total.get("sent", 0) + len(engines[c])
        g.remote_dma_fused(tr, local_sem=sem.sent)

    fill("nxrow", T.nxrow[:], 0)
    for k in range(8):
        dma("s", "dst", "", "stw", T.stw[16 * k:16 * k + 16, :], T.st[:])
        dma("y", "dbt", "", "btw", T.btw[16 * k:16 * k + 16, :], T.bt[:])
    for k in range(2):
        dma("s", "dnw", "", "nxw", T.nxw[16 * k:16 * k + 16, :], T.nx[:])
    dma("y", "dnx", "", "nxrow", T.nxrow[0:1, :], T.nx[:])
    dma("y", "dx", "", "xt", T.xt[:], T.x[:])

    ic, ict, cf, fw = T.ic, T.ict, T.cf, T.fw
    iota("ic", ic[:, 0:32], [[0, 2], [512, 8], [0, 2]], 0)
    iota("ic", ic[:, 32:64], [[8, 2], [0, 8], [128, 2]], 4, 1)
    iota("ic", ic[:, 64:96], [[1, 2], [0, 16]], 0)
    iota("ic", ic[:, 96:128], [[0, 2], [1, 16]], 0)
    iota("ic", ic[:, 128:160], [[1, 32]], 0)
    iota("kL", T.kL[:], [[16384, 208]], 0)
    iota("ioL0", T.ioL[:, 0:256], [[1, 256]], 0)
    iota("wab", T.wab[:], [[32, 20], [0, 2]], 0)
    iota("cw0", T.cw0[:], [[16, 40]], 0)
    turn("ic", "ict", ict[:], ic[:])
    f = lambda j: cf[:, j:j + 1]
    lo, odd, q15, q31 = (ict[:, j:j + 1] for j in (0, 64, 96, 128))
    ts("ict", "hi", f(1), lo, 512.0, A.add)
    ts("ict", "sb", f(2), ict[:, 32:33], -0.125, A.mult)
    ts("ict", "sb", f(3), ict[:, 32:33], -0.125, A.mult, -2.0, A.add)
    ts("ict", "nbc", f(4), lo, -2.0, A.mult, -16384.0 * 96, A.add)

    o1 = T.o1
    ts("btw", "b0", o1[:, 0:12], T.btw[:], 1, A.bitwise_and)
    ts("stw", "e0", o1[:, 24:36], T.stw[:], 2, A.mult)
    tt("e0 b0", "e1", o1[:, 36:48], o1[:, 24:36], o1[:, 0:12], A.add)
    ts("e1", "e2", o1[:, 48:60], o1[:, 36:48], 1025, A.mult)
    ts("e2", "e3", o1[:, 24:36], o1[:, 48:60], 4, A.arith_shift_right, 1023, A.bitwise_and)
    copy("e3", "off1", T.off1[:], o1[:, 24:36])
    copy("nxrow off1", "n1r", T.n1r[:], T.nxrow[:].indirect(T.off1[:]))
    op("g", "n1r", "n1L", lambda e: e.partition_broadcast(T.n1L[:], T.n1r[0:1, :], 128))
    copy("nxw", "nxf", T.nxf[0:32, :], T.nxw[0:32, :])
    turn("nxf", "nxt", T.nxt[0:32, :], T.nxf[0:32, :])
    for b in range(2):
        dma("y", "dnl", "nxt", "nxlin", T.nxlin[0:1, 512 * b:512 * b + 512], T.nxt[0:32, 32 * b:32 * b + 16])
    op("g", "nxlin", "nxl", lambda e: e.partition_broadcast(T.nxl[:, 0:1024], T.nxlin[0:1, :], 128))
    iota("nxl", T.nxl[:, 1024:1032], [[0, 8]], N * TN)
    ts("btw", "b1", o1[:, 12:24], T.btw[:], 1, A.arith_shift_right)
    copy("b1", "b1u", T.b1u[:], o1[:, 12:24])
    copy("ioL0 b1u", "b1L", T.b1L[:], T.ioL[:, 0:8].indirect(T.b1u[:]))
    tt("b1L kL", "kb", T.kb[:], T.b1L[:], T.kL[:, 0:V], A.add)
    ts("n1L ict", "ga", T.ga[:], T.n1L[:], lo, A.is_ge)
    ts("n1L hi", "gb", T.gb[:], T.n1L[:], f(1), A.is_ge)
    scan("ga gb", "c1L", T.c1L[:], T.ga[:], T.gb[:], 0.0, A.subtract)
    copy("n1L", "a1", T.a1[:], T.n1L[:], q="s", scale=2.0)
    for k in range(2):
        count("c1L sb", "cnt1 sgx%d" % k, T["sg%d" % k][:], T.c1L[:], f(2 + k), T.cnt1[:, k:k + 1])
    tt("a1 kb", "aL", T.aL[:, 0:V], T.a1[:], T.kb[:], A.add)
    ts("ict", "nsc", f(5), lo, 2.0, A.mult, 1024.0, A.add)
    ts("kL nsc", "aL", T.aL[:, V:208], T.kL[:, V:208], f(5), A.add)
    ts("cnt1 nbc", "nb", T.nb[:], T.cnt1[:], 8192.0, A.mult, f(4), A.add)
    op("s", "aL nb", "ab1", lambda e: e.activation(T.ab1[:], T.aL[:], F.Abs, bias=T.nb[:, 1:2]))
    ts("aL nb", "sub0", T.sub0[:], T.aL[:], T.nb[:, 0:1], A.add)
    ts("cnt1", "pk", T.pk[:], T.cnt1[:], -1024.0, A.mult, 2048.0 * (96 + V * r), A.add)
    op("v", "sub0", "vv", lambda e: e.tensor_reduce(T.vv[:, 0:1], T.sub0[:], AxisListType.X, A.min, apply_absolute_value=True))
    fill("x1", T.x1[:], 0.0)
    op("v", "ab1", "vv", lambda e: e.tensor_reduce(T.vv[:, 1:2], T.ab1[:], AxisListType.X, A.min))
    tt("pk vv", "x1", T.x1[:, 0:64:32], T.pk[:], T.vv[:], A.add)
    turn("x1", "x1t", T.x1t[:], T.x1[:])
    for k in range(8):
        dma("y" if k % 2 else "s", "dc1", "x1t", "w1", T.w1[16 * k:16 * k + 16, :], T.x1t[0:128:32, :])
    send("w1", "al1", lambda d: T.w1[:, 2 * d:2 * d + 2], lambda j: T.land1[:, 2 * j:2 * j + 2])

    ts("wab ict", "wac", T.wac[:], T.wab[:], q31, A.add)
    copy("n1L wac", "own", T.own[:], T.n1L[:].indirect(T.wac[:, 0:12]), q="s")
    ts("cw0 ict", "cw", T.cw[:], T.cw0[:], q15, A.add)
    ts("ict", "even", f(6), odd, -1.0, A.mult, 1.0, A.add)
    ts("cw", "dw", T.dw[:], T.cw[:], float(KEYS), A.add)
    ts("cw", "kw", fw[:, 0:12], T.cw[:, 0:12], float(V * r), A.add)
    copy("stw", "stu", T.stu[:], T.stw[:])
    op("v", "xt", "xq xs", lambda e: e.quantize_mx(T.xq[:], T.xs[:], T.xt[:]))
    pick("xq", "xs", "stq", "sts", T.stq[:], T.sts[:], T.xq[:], T.xs[:], T.stu[:], "stu")
    turn("own", "ownt", T.ownt[:], T.own[:])
    copy("w1", "w1i", T.w1i[:], T.w1[:])
    ts("w1i", "w1k", T.w1k[:], T.w1i[:], 11, A.arith_shift_right)
    ts("w1k", "s1off", T.s1off[:], T.w1k[:], -V * r, A.add, V - 1, A.min)
    pick("stq", "sts", "p1q", "p1s", T.p1q[:], T.p1s[:], T.stq[:], T.sts[:], T.s1off[:], "s1off")
    send("p1q", "aq1", lambda d: T.p1q[:, CAP * d:CAP * d + CAP].bitcast(dt.uint8),
         lambda j: T.cq[:, V + CAP * j:V + CAP * j + CAP].bitcast(dt.uint8))
    send("p1s", "as1", lambda d: T.p1s[:, CAP * d:CAP * d + CAP], lambda j: T.cs[:, V + CAP * j:V + CAP * j + CAP])
    dma("y", "dcq", "stq", "cq0", T.cq[:, 0:V].bitcast(dt.uint8), T.stq[:].bitcast(dt.uint8))
    dma("y", "dcq", "sts", "cs0", T.cs[:, 0:V], T.sts[:])
    dma("y", "dw_", "", "wt", T.wt[:], T.w[:])
    iota("keyL", T.keyL[:, 0:V], [[1, V]], V * r)
    iota("infoX", T.infoL[:, CAND:CX], [[1, CAP]], KEYS + CAND + CAP * r)
    iota("ioL", T.ioL[:, 256:KW], [[1, KW - 256]], 256)
    iota("ones", T.ones[:], [[0, CAND]], 1)
    iota("sT", T.sT[:, 0:KEYS], [[1, 8], [0, V]], 0)
    iota("sT", T.sT[:, KEYS:KW], [[0, 8]], 0)
    iota("iT", T.iT[:, KEYS:KW], [[0, 8]], 0)
    ow = T.ow
    copy("ownt", "n1w", ow[:, 0:12], T.ownt[:, 0:V:16])
    ts("n1w", "oc", ow[:, 12:24], ow[:, 0:12], 511, A.bitwise_and)
    ts("n1w", "oa", ow[:, 24:36], ow[:, 0:12], 9, A.arith_shift_right)
    ts("oc", "od", ow[:, 36:48], ow[:, 12:24], 2, A.mult)
    ts("oa", "of", ow[:, 48:60], ow[:, 24:36], r, A.not_equal, 2048, A.mult)
    tt("od b1", "oe", ow[:, 60:72], ow[:, 36:48], o1[:, 12:24], A.add)
    copy("oc", "c1u0", T.c1u[:, 0:12], ow[:, 12:24])
    tt("oe of", "og", ow[:, 72:84], ow[:, 60:72], ow[:, 48:60], A.add)
    ts("og", "noff0", T.noff[:, 0:12], ow[:, 72:84], 1024, A.min)
    copy("nxl noff0", "n2L0", T.n2L[:, 0:V], T.nxl[:].indirect(T.noff[:, 0:12]))
    ts("n2L0 ict", "g2a0", T.g2a[:, 0:V], T.n2L[:, 0:V], lo, A.is_ge)
    ts("n2L0 hi", "g2b0", T.g2b[:, 0:V], T.n2L[:, 0:V], f(1), A.is_ge)
    scan("g2a0 g2b0", "c2L0", T.c2L[:, 0:V], T.g2a[:, 0:V], T.g2b[:, 0:V], 0.0, A.subtract)
    for k in range(2):
        count("c2L0 sb", "cnt2o sgy%d" % k, T["sg%d" % (2 + k)][:, 0:V], T.c2L[:, 0:V], f(2 + k), T.cnt2[:, k:k + 1])
    copy("n2L0", "inf00", T.inf0[:, 0:V], T.n2L[:, 0:V], q="s", scale=4096.0)
    fill("x2", T.x2[:], 0.0)

    wrote["land1"] = [arrivals("al1")]
    wrote["cqa"] = [arrivals("aq1")]
    wrote["csa"] = [arrivals("as1")]
    l1 = T.l1
    copy("land1", "l1", l1[:, 0:14], T.land1[:])
    ts("l1", "la", l1[:, 14:28], l1[:, 0:14], 2047, A.bitwise_and)
    copy("la", "noff1", T.noff[:, 12:26], l1[:, 14:28])
    copy("nxl noff1", "n2L1", T.n2L[:, V:CAND], T.nxl[:].indirect(T.noff[:, 12:26]))
    ts("n2L1 ict", "g2a1", T.g2a[:, V:CAND], T.n2L[:, V:CAND], lo, A.is_ge)
    ts("n2L1 hi", "g2b1", T.g2b[:, V:CAND], T.n2L[:, V:CAND], f(1), A.is_ge)
    scan("g2a1 g2b1 c2L0", "c2L1", T.c2L[:, V:CAND], T.g2a[:, V:CAND], T.g2b[:, V:CAND], T.c2L[:, V - 1:V], A.subtract)
    ts("ioL0 c2L1", "c2L2", T.c2L[:, CAND:CX], T.ioL[:, 1:1 + CAP], T.c2L[:, CAND - 1:CAND], A.add)
    for k in range(2):
        count("c2L1 c2L2 sb", "cnt2a sgz%d" % k, T["sg%d" % (2 + k)][:, V:CX], T.c2L[:, V:CX], f(2 + k), T.cnt2[:, 4 + k:5 + k])
    ts("cnt2o", "cnt2h", T.cnt2[:, 2:4], T.cnt2[:, 0:2], -0.5, A.mult, CX / 2.0, A.add)
    ts("l1", "lk", l1[:, 28:42], l1[:, 0:14], 11, A.arith_shift_right)
    ts("l1", "le", l1[:, 42:56], l1[:, 0:14], 1, A.arith_shift_right, 511, A.bitwise_and)
    copy("lk", "ku1", T.ku1[:], l1[:, 28:42])
    ts("cnt2a", "cnt2b", T.cnt2[:, 6:8], T.cnt2[:, 4:6], -0.5, A.mult)
    tt("cnt2b cnt2h", "x2", T.x2[:, 0:64:32], T.cnt2[:, 6:8], T.cnt2[:, 2:4], A.add)
    turn("x2", "x2t", T.x2t[:], T.x2[:])
    for k in range(8):
        dma("y" if k % 2 else "s", "dc2", "x2t", "w2", T.w2[16 * k:16 * k + 16, :], T.x2t[0:128:32, :])
    copy("n2L1", "inf01", T.inf0[:, V:CAND], T.n2L[:, V:CAND], q="s", scale=4096.0)
    copy("ioL0 ioL ku1", "keyL1", T.keyL[:, V:CAND], T.ioL[:].indirect(T.ku1[:]), q="s")
    tt("inf00 keyL", "info0", T.infoL[:, 0:V], T.inf0[:, 0:V], T.keyL[:, 0:V], A.add)
    copy("le", "c1u1", T.c1u[:, 12:26], l1[:, 42:56])
    tt("inf01 keyL1", "info1", T.infoL[:, V:CAND], T.inf0[:, V:CAND], T.keyL[:, V:CAND], A.add)
    pick("xq", "xs", "cq1", "cs1", T.cq[:, CAND:2 * CAND], T.cs[:, CAND:2 * CAND], T.xq[:], T.xs[:], T.c1u[:], "c1u0 c1u1")
    copy("w2", "w2u", T.w2u[:], T.w2[:])
    copy("info0 info1 infoX w2u", "ig", T.ig[:], T.infoL[:].indirect(T.w2u[:]))
    copy("ig wac", "ig2", T.ig2[:], T.ig[:].indirect(T.wac[:, 0:16]))
    turn("ig2", "igt", T.igt[:], T.ig2[:])
    copy("igt", "l2s", T.l2s[:], T.igt[:, 0:256:16])
    send("l2s", "al2", lambda d: T.l2s[:, 2 * d:2 * d + 2], lambda j: T.land2[:, 2 * j:2 * j + 2])
    ts("w2", "o2off", T.o2off[:, 0:32:2], T.w2[:], CAND - 1.0, A.min)
    ts("w2", "o2off", T.o2off[:, 1:32:2], T.w2[:], CAND - 1.0, A.min, float(CAND), A.add)
    pick("cq0 cq1 cqa", "cs0 cs1 csa", "p2q", "p2s", T.p2q[:], T.p2s[:], T.cq[:], T.cs[:], T.o2off[:], "o2off")
    send("p2q", "aq2", lambda d: T.p2q[:, 64 * d:64 * d + 64].bitcast(dt.uint8),
         lambda j: T.eq[:, 64 * j:64 * j + 64].bitcast(dt.uint8))
    send("p2s", "as2", lambda d: T.p2s[:, 64 * d:64 * d + 64], lambda j: T.es[:, 64 * j:64 * j + 64])
    iota("pp", T.pp[:, KEYS:KEYS + TAIL], [[1, TAIL]], M + 1)
    iota("yx", T.yx[:, 0:CAND], [[1, CAND]], 0)
    iota("yx", T.yx[:, CAND:ALL], [[32, 14], [1, 16]], CAND)
    iota("inv", T.inv[:, 0:M], [[0, M]], YZ)
    iota("iT", T.iT[:, 0:KEYS], [[0, 8], [1, V]], 0)
    for o in range(2):
        iota("ybz%d" % o, T["yb%d" % o][:, YZ:YZ + 8], [[0, 8]], 0)
    iota("sW", T.sW[:, 0:V], [[0, V]], r)
    iota("iW", T.iW[:, 0:V], [[1, V]], 0)
    iota("sW", T.sW[:, YZ:YZ + 8], [[0, 8]], -1)
    iota("iW", T.iW[:, YZ:YZ + 8], [[0, 8]], -1)

    n2w, xx = T.n2w, T.xx
    copy("n2L0 n2L1 wac", "n2g", T.n2g[:], T.n2L[:].indirect(T.wac[:, 0:26]), q="s")
    copy("ioL0 ioL", "bm", T.bm[:, 0:KEYS], T.ioL[:, 0:KEYS], q="s", scale=0.0)
    copy("lk", "kw", fw[:, 12:26], l1[:, 28:42])
    turn("n2g", "n2t", T.n2t[:], T.n2g[:])
    copy("n2t", "n2w", n2w[:, 0:26], T.n2t[:, 0:CAND:16])
    ts("n2w", "n2e", n2w[:, 52:78], n2w[:, 0:26], 9, A.arith_shift_right)
    ts("n2w", "n2c", n2w[:, 26:52], n2w[:, 0:26], 511, A.bitwise_and)
    ts("n2e", "bad", fw[:, 26:52], n2w[:, 52:78], r, A.not_equal)
    copy("n2c", "c2u", T.c2u[:], n2w[:, 26:52])
    tt("bad dw", "badd", fw[:, 52:78], fw[:, 26:52], T.dw[:, 0:26], A.mult)
    pick("xq", "xs", "n2q", "n2s", T.n2q[:], T.n2s[:], T.xq[:], T.xs[:], T.c2u[:], "c2u")
    tt("kw badd", "ko", T.ko[:], fw[:, 0:26], fw[:, 52:78], A.max)
    op("v", "wt", "wq0 ws0", lambda e: e.quantize_mx(T.wq[:, 0:384], T.ws[:, 0:384], T.wt[:, 0:1536]))
    copy("ko", "kou0", T.kou[:, 0:26], T.ko[:])
    op("v", "wt", "wq1 ws1", lambda e: e.quantize_mx(T.wq[:, 384:768], T.ws[:, 384:768], T.wt[:, 1536:3072]))
    op("v", "kou0 ones", "bm", lambda e: e.tensor_copy(T.bm[:].indirect(T.kou[:, 0:26]), T.ones[:]))
    ts("ko even", "qa", xx[:, 0:13], T.ko[:, 0:26:2], f(6), A.mult)
    ts("ko ict", "qb", xx[:, 13:26], T.ko[:, 1:26:2], odd, A.mult)
    tt("qa qb", "qc", xx[:, 26:39], xx[:, 0:13], xx[:, 13:26], A.add)
    copy("qc", "pwa", T.pwa[:, 0:26:2], xx[:, 26:39])
    copy("qc", "pwa", T.pwa[:, 1:26:2], xx[:, 26:39])

    W = lambda k, o: (T.wq[:, 128 * (2 * k + o):128 * (2 * k + o) + 128], T.ws[:, 128 * (2 * k + o):128 * (2 * k + o) + 128])

    def mm(r_, w_, bank, n, k, o, q, s, a, b):
        wq, ws = W(k, o)
        op("t", r_ + " wq0 ws0 wq1 ws1", w_, lambda e: e.matmul_mx(T.ps[:, 512 * bank:512 * bank + n], wq, ws, q, s, a, b))

    for o in range(2):
        mm("cq0 cqa cs0 csa", "psS%d" % o, o, CAND, 0, o, T.cq[:, 0:CAND], T.cs[:, 0:CAND], True, False)
        mm("cq1 cs1", "psS%d" % o, o, CAND, 1, o, T.cq[:, CAND:2 * CAND], T.cs[:, CAND:2 * CAND], False, False)
        mm("n2q n2s", "psS%d" % o, o, CAND, 2, o, T.n2q[:], T.n2s[:], False, True)

    wrote["land2"] = [arrivals("al2")]
    wrote["eqa"] = [arrivals("aq2")]
    wrote["esa"] = [arrivals("as2")]
    l2 = T.l2i
    copy("land2", "m0", l2[:, 0:14], T.land2[:])
    ts("m0", "m1", l2[:, 14:28], l2[:, 0:14], 4095, A.bitwise_and)
    copy("m1", "kou1", T.kou[:, 26:40], l2[:, 14:28])
    op("v", "kou1 ones", "bm", lambda e: e.tensor_copy(T.bm[:].indirect(T.kou[:, 26:40]), T.ones[:, 0:ARR]))
    ts("m0", "m2", l2[:, 28:42], l2[:, 0:14], 12, A.arith_shift_right, 511, A.bitwise_and)
    ts("m1 even", "qd", xx[:, 39:46], l2[:, 14:28:2], f(6), A.mult)
    ts("m1 ict", "qe", xx[:, 46:53], l2[:, 15:28:2], odd, A.mult)
    scan("bm", "pp", T.pp[:, 0:KEYS], T.bm[:, 0:KEYS], T.bm[:, 0:KEYS], 0.0, A.max)
    tt("qd qe", "qf", xx[:, 53:60], xx[:, 39:46], xx[:, 46:53], A.add)
    copy("m2", "c2ua", T.c2ua[:, 0:28:2], l2[:, 28:42])
    copy("qf", "pwb", T.pwa[:, 26:40:2], xx[:, 53:60])
    copy("qf", "pwb", T.pwa[:, 27:40:2], xx[:, 53:60])
    copy("m2", "c2ua", T.c2ua[:, 1:28:2], l2[:, 28:42])
    copy("pp pwa", "pg0", T.pg[:, 0:320], T.pp[:].indirect(T.pwa[:, 0:20]))
    copy("pp pwa pwb", "pg1", T.pg[:, 320:ALL], T.pp[:].indirect(T.pwa[:, 20:40]), q="s")
    turn("pg0", "pt0", T.pt[:, 0:320], T.pg[:, 0:320])
    ts("m1", "ku2", T.ku2[:, 0:28:2], l2[:, 14:28], KEYS - 1, A.min)
    ts("m1", "ku2", T.ku2[:, 1:28:2], l2[:, 14:28], KEYS - 1, A.min)
    turn("pg1", "pt1", T.pt[:, 320:ALL], T.pg[:, 320:ALL])
    ts("pt0 pt1", "plu", T.plu[:], T.pt[:, 0:ALL:16], -1.0, A.add)
    pick("xq", "xs", "fq", "fs", T.fq[:], T.fs[:], T.xq[:], T.xs[:], T.c2ua[:, 0:27], "c2ua")
    op("v", "plu yx", "inv", lambda e: e.tensor_copy(T.inv[:].indirect(T.plu[:]), T.yx[:]))
    copy("inv wac", "ivg", T.ivg[:], T.inv[:, 0:M].indirect(T.wac[:, 0:18]))
    turn("ivg", "ivt", T.ivt[:], T.ivg[:])
    copy("ivt", "ylu", T.ylu[:], T.ivt[:, 0:M:16])
    for o in range(2):
        mm("fq fs", "psA%d" % o, 2 + o, SPREAD, 2, o, T.fq[:], T.fs[:], True, False)
    for o in range(2):
        copy("psS%d" % o, "yb%d" % o, T["yb%d" % o][:, 0:CAND], T.ps[:, 512 * o:512 * o + CAND], q="s")
    for t_, w_ in (("sT", "sW"), ("iT", "iW")):
        copy(t_ + " ku1", w_, T[w_][:, V:CAND], T[t_][:].indirect(T.ku1[:]), q="s")
        copy(t_ + " ku2", w_, T[w_][:, CAND:YZ], T[t_][:].indirect(T.ku2[:, 0:27]), q="s")
    for o in range(2):
        mm("eqa esa", "psA%d" % o, 2 + o, SPREAD, 0, o, T.eq[:, 0:SPREAD], T.es[:, 0:SPREAD], False, False)
        mm("eqa esa", "psA%d" % o, 2 + o, SPREAD, 1, o, T.eq[:, 16:16 + SPREAD], T.es[:, 16:16 + SPREAD], False, True)
    copy("psA0", "yb0", T.yb0[:, CAND:YZ], T.ps[:, 1024:1024 + SPREAD], q="s")
    copy("psA1", "yb1", T.yb1[:, CAND:YZ], T.ps[:, 1536:1536 + SPREAD], q="s")
    copy("yb0 ybz0 ylu", "yo0", T.yo0[:], T.yb0[:].indirect(T.ylu[:]))
    dma("y", "dy0", "yo0", "y0", T.y[:, 0:M], T.yo0[:])
    copy("yb1 ybz1 ylu", "yo1", T.yo1[:], T.yb1[:].indirect(T.ylu[:]), q="s")
    dma("s", "dy1", "yo1", "y1", T.y[:, M:2 * M], T.yo1[:])
    copy("sW ylu", "ids", T.ids[:], T.sW[:].indirect(T.ylu[:]))
    dma("y", "did", "ids", "id0", T["id"][0:1, :], T.ids[0:1, :])
    copy("iW ylu", "idi", T.idi[:], T.iW[:].indirect(T.ylu[:]), q="s")
    dma("s", "did2", "idi", "id1", T["id"][1:2, :], T.idi[0:1, :])
    await_("g", [(s, None) for s in total])
